import numpy as np
import ml_dtypes


def mxq(x, axis, fmt="e4m3"):
    dtype, down = {"e4m3": (ml_dtypes.float8_e4m3fn, 7), "e5m2": (ml_dtypes.float8_e5m2, 14)}[fmt]
    v = np.moveaxis(np.asarray(x, np.float32).astype(ml_dtypes.bfloat16).astype(np.float64), axis, -1)
    blocks = v.reshape(v.shape[:-1] + (-1, 32))
    amax = np.abs(blocks).max(-1, keepdims=True)
    byte = np.maximum(np.where(amax > 0, np.frexp(amax)[1] - 1 + 127, 0) - down, 1)
    scale = np.exp2(byte - 127.0)
    codes = (blocks / scale).astype(np.float32).astype(dtype).astype(np.float64)
    return np.moveaxis((codes * scale).reshape(v.shape), -1, axis)


WIDE = False


def mx_kscale(k):
    if not WIDE:
        return np.ones(k)
    levels = np.array([10, -10, 5, -5, 0])
    if k % 512:
        return np.exp2(np.random.permutation(np.resize(levels, k // 32))).repeat(32)
    a = np.empty((k // 512, 16))
    for p in range(k // 512):
        a[p, :8] = np.random.permutation(np.resize(levels, 8))
        for g in range(8):
            far = levels[np.abs(levels - a[p, g]) >= 10]
            a[p, g + 8] = far[np.random.randint(len(far))]
    return np.exp2(a.ravel()).repeat(32)


def f64(x):
    return np.asarray(x).astype(np.float64)


def striped(idx):
    return np.tile(idx.reshape(-1, 16).T, (8, 1)).astype(np.uint16)


def unstriped(offs):
    return offs[:16].T.reshape(-1).astype(np.int64)


E2M1 = np.array([0.0, 0.5, 1.0, 1.5, 2.0, 3.0, 4.0, 6.0, -0.0, -0.5, -1.0, -1.5, -2.0, -3.0, -4.0, -6.0])


def pack_weight(w, fmt):
    k, n = w.shape
    w = f64(np.asarray(w, np.float32).astype(ml_dtypes.bfloat16)).reshape(k // 32, 32, n)
    amax = np.abs(w).max(1)
    if fmt == "e4m3":
        byte = np.frexp(amax)[1] - 1 + 127 - 7
    else:
        mant, ex = np.frexp(amax / 6.0)
        byte = np.where(mant > 0.5, ex, ex - 1) + 127
    byte = np.clip(np.where(amax > 0, byte, 1), 1, 254)
    scaled = (w * np.exp2(127.0 - byte)[:, None, :]).reshape(k, n).astype(np.float32)
    by_word = np.ascontiguousarray(scaled.reshape(k // 512, 128, 4, n).transpose(0, 1, 3, 2))
    if fmt == "e4m3":
        words = by_word.astype(ml_dtypes.float8_e4m3fn).view(np.uint8)
    else:
        c = by_word.astype(ml_dtypes.float4_e2m1fn).view(np.uint8) & 0xF
        words = (c[..., 0::2] | (c[..., 1::2] << 4)).reshape(k // 512, 128, 2 * n)
    return np.ascontiguousarray(words), np.ascontiguousarray(byte.astype(np.uint8).reshape(k // 512, 16, n))


def unpack_weight(words, scales, fmt):
    g, _, n = scales.shape
    words = np.ascontiguousarray(words).reshape(g, 128, n, -1)
    if fmt == "e4m3":
        vals = words.view(ml_dtypes.float8_e4m3fn).astype(np.float64)
    else:
        nib = np.empty((g, 128, n, 4), np.uint8)
        nib[..., 0::2] = words & 0xF
        nib[..., 1::2] = words >> 4
        vals = E2M1[nib]
    vals = vals * np.repeat(np.exp2(scales.astype(np.float64) - 127.0), 8, axis=1)[..., None]
    return vals.transpose(0, 1, 3, 2).reshape(g * 512, n)


def silu(v):
    return v / (1.0 + np.exp(-np.maximum(v, -700.0)))


def d_silu(v):
    s = 1.0 / (1.0 + np.exp(-np.maximum(v, -700.0)))
    return s * (1.0 + v * (1.0 - s))


K, T, E, C, H, N = 768, 512, 4, 256, 512, 1024


def by_expert(wq, xq):
    return np.concatenate([wq[e].T @ xq[:, e * C:(e + 1) * C] for e in range(E)], axis=1)


def setup_inputs():
    n = np.random.standard_normal
    s = mx_kscale(N)[:, None]
    u = mx_kscale(H)
    first = np.random.permutation(np.repeat(np.arange(E), T // E))
    second = (first + 1 + np.random.permutation(np.repeat(np.arange(E - 1), -(-T // (E - 1)))[:T])) % E
    while np.bincount(second, minlength=E).max() != T // E:
        load = np.bincount(second, minlength=E); hi, lo = int(load.argmax()), int(load.argmin())
        t = np.flatnonzero((second == hi) & (first != lo))[0]; second[t] = lo
    slot_token = np.empty(E * C, np.int64); pos = np.empty((2, T), np.int64); fill = np.zeros(E, np.int64)
    place = np.stack([np.random.permutation(C) for _ in range(E)])
    for r, deal in enumerate((first, second)):
        for t in np.random.permutation(T):
            e = deal[t]; j = e * C + place[e, fill[e]]; fill[e] += 1; slot_token[j] = t; pos[r, t] = j
    g = np.random.uniform(0.2, 0.8, T)
    w_slot = np.empty(E * C); w_slot[pos[0]] = g; w_slot[pos[1]] = 1.0 - g
    w2 = [pack_weight(m, "e2m1") for m in n((E, N, H)) / np.sqrt(N) / s[None] * u[None, None, :]]
    w1 = [pack_weight(m, "e2m1") for m in n((E, H, K)) / np.sqrt(H) / u[None, :, None]]
    w3 = [pack_weight(m, "e2m1") for m in n((E, H, K)) / np.sqrt(H) / u[None, :, None]]
    return {
        "dyT": (n((N, T)) * s).astype(np.float32),
        "a1": n((H, E * C)).astype(np.float32),
        "a3": n((H, E * C)).astype(np.float32),
        "w2_words": np.stack([m[0] for m in w2]),
        "w2_scales": np.stack([m[1] for m in w2]),
        "w1_words": np.stack([m[0] for m in w1]),
        "w1_scales": np.stack([m[1] for m in w1]),
        "w3_words": np.stack([m[0] for m in w3]),
        "w3_scales": np.stack([m[1] for m in w3]),
        "gate": np.tile(w_slot, (N, 1)).astype(np.float32),
        "offs": striped(slot_token),
        "pos1": striped(pos[0]),
        "pos2": striped(pos[1]),
    }


def reference(dyT, a1, a3, w2_words, w2_scales, w1_words, w1_scales, w3_words, w3_scales, gate, offs, pos1, pos2):
    idx = unstriped(offs)
    w2 = np.stack([unpack_weight(w2_words[e], w2_scales[e], "e2m1") for e in range(E)])
    w1 = np.stack([unpack_weight(w1_words[e], w1_scales[e], "e2m1") for e in range(E)])
    w3 = np.stack([unpack_weight(w3_words[e], w3_scales[e], "e2m1") for e in range(E)])
    gq = mxq(f64(gate) * f64(dyT)[:, idx], 0, "e4m3")
    dh = by_expert(w2, gq)
    da1 = dh * f64(a3) * d_silu(f64(a1))
    da3 = dh * silu(f64(a1))
    dx = by_expert(w1, mxq(da1, 0, "e4m3")) + by_expert(w3, mxq(da3, 0, "e4m3"))
    return dx[:, unstriped(pos1)] + dx[:, unstriped(pos2)]

@@ -1,0 +1,295 @@
+from contextlib import ExitStack
+
+import concourse.mybir as mybir
+from concourse.masks import make_identity
+
+K, T, E, C, H, N = 768, 512, 4, 256, 512, 1024
+S = E * C
+
+FLOPS = 2 * S * (N * H + 2 * H * K)
+BYTES = 4 * (N * T + 2 * H * S + S + K * T) + E * (N * H // 2 + N * H // 32) + 2 * E * (H * K // 2 + H * K // 32) + 2 * (S + 2 * T) * 8
+
+F32 = mybir.dt.float32
+BF16 = mybir.dt.bfloat16
+U32 = mybir.dt.uint32
+I32 = mybir.dt.int32
+U16 = mybir.dt.uint16
+U8 = mybir.dt.uint8
+E4M3X4 = mybir.dt.float8_e4m3fn_x4
+E2M1X4 = mybir.dt.float4_e2m1fn_x4
+ACT = mybir.ActivationFunctionType
+MULT = mybir.AluOpType.mult
+SUB = mybir.AluOpType.subtract
+ADD = mybir.AluOpType.add
+
+P = 128
+HALF = 128
+NPASS = N // 512
+KT = K // P
+CUTS = ((0, 256), (256, 384), (640, 384))
+
+
+def tile_moe_bdx_glu_silu_kernel(
+    tc, dyT, a1, a3, w2_words, w2_scales, w1_words, w1_scales, w3_words, w3_scales, gate, offs, pos1, pos2, out
+):
+    nc = tc.nc
+    with ExitStack() as ctx:
+        keep = ctx.enter_context(tc.tile_pool(name="keep", bufs=1))
+        ring3 = ctx.enter_context(tc.tile_pool(name="ring3", bufs=3))
+        ring2 = ctx.enter_context(tc.tile_pool(name="ring2", bufs=2))
+        psum = ctx.enter_context(tc.psum_pool(name="psum", bufs=2))
+
+        offs_t = keep.tile([P, S // 16], U16, name="offs_t")
+        pos1_t = keep.tile([P, T // 16], U16, name="pos1_t")
+        pos2_t = keep.tile([P, T // 16], U16, name="pos2_t")
+        dy = [[keep.tile([P, T], F32, name=f"dy{s}{t}") for t in range(4)] for s in range(NPASS)]
+        gate_t = keep.tile([P, S], F32, name="gate_t")
+        a1_t = [keep.tile([P, 4, 2 * C], F32, name=f"a1_t{i}") for i in range(2)]
+        a3_t = [keep.tile([P, 4, C], F32, name=f"a3_t{e}") for e in range(E)]
+        w2_t = keep.tile([P, E * NPASS, 2 * H], U8, name="w2_t", align_bytes=64)
+        w2s_t = keep.tile([P, E * NPASS, H], U8, name="w2s_t", align_bytes=64)
+        w13_t = [keep.tile([P, E, 2 * K], U8, name=f"w13_t{j}", align_bytes=64) for j in range(2)]
+        w13s_t = [keep.tile([P, E, K], U8, name=f"w13s_t{j}", align_bytes=64) for j in range(2)]
+        ident = keep.tile([P, P], F32, name="ident")
+        dummy = keep.tile([P, 1], F32, name="dummy")
+
+        nc.gpsimd.memset(w2s_t[:].bitcast(I32), 0)
+        nc.gpsimd.memset(w13s_t[0][:].bitcast(I32), 0)
+        nc.gpsimd.memset(w13s_t[1][:].bitcast(I32), 0)
+        make_identity(nc, ident[:])
+
+        def load_dy(s, t):
+            rows = dyT[512 * s : 512 * (s + 1), :].rearrange("(p t) n -> t p n", t=4)
+            nc.sync.dma_start(out=dy[s][t][:], in_=rows[t])
+
+        def load_w2(e):
+            src = w2_words.bitcast(I32).rearrange("e s p n -> p (e s) n")
+            es = slice(e * NPASS, (e + 1) * NPASS)
+            nc.sync.dma_start(out=w2_t[:, es, :].bitcast(I32), in_=src[:, es, :])
+
+        def load_scales(dst, src):
+            view = src.bitcast(I32).rearrange("e s (q r) i -> r q (e s) i", r=4)
+            for r in range(4):
+                nc.sync.dma_start(out=dst[:].bitcast(I32)[r : P : 32, :, :], in_=view[r])
+
+        def load_a(dst, src, e):
+            cols = slice(e * C, (e + 1) * C)
+            nc.sync.dma_start(out=dst[e][:], in_=src.rearrange("(p t) n -> p t n", t=4)[:, :, cols])
+
+        def load_a1(i):
+            cols = slice(2 * i * C, 2 * (i + 1) * C)
+            nc.sync.dma_start(out=a1_t[i][:], in_=a1.rearrange("(p t) n -> p t n", t=4)[:, :, cols])
+
+        def load_gate(e):
+            nc.sync.dma_start(out=gate_t[:, e * C : (e + 1) * C], in_=gate[0:P, e * C : (e + 1) * C])
+
+        nc.vector.memset(dummy[:], 0.0)
+        nc.scalar.activation(dummy[:], dummy[:], ACT.Silu)
+
+        nc.scalar.dma_start(out=gate_t[:, 0:C], in_=gate[0:P, 0:C])
+        nc.sync.dma_start(offs_t[:], offs)
+        load_dy(0, 0)
+        for e in range(1, E):
+            load_gate(e)
+        load_dy(0, 1)
+        load_a1(0)
+        load_dy(0, 2)
+        load_dy(0, 3)
+        load_a1(1)
+        for t in range(4):
+            load_dy(1, t)
+        load_w2(0)
+        load_scales(w2s_t, w2_scales)
+        load_w2(1)
+        load_a(a3_t, a3, 0)
+        load_w2(2)
+        load_w2(3)
+        load_a(a3_t, a3, 1)
+        for j, (words, scales) in enumerate(((w1_words, w1_scales), (w3_words, w3_scales))):
+            nc.sync.dma_start(out=w13_t[j][:].bitcast(I32), in_=words.bitcast(I32).rearrange("e s p n -> p (e s) n"))
+            load_scales(w13s_t[j], scales)
+        load_a(a3_t, a3, 2)
+        load_a(a3_t, a3, 3)
+        nc.sync.dma_start(pos1_t[:], pos1)
+        nc.sync.dma_start(pos2_t[:], pos2)
+
+        codes = keep.tile([P, NPASS, S], U32, name="codes", align_bytes=64)
+        scales_g = keep.tile([P, NPASS, S], U8, name="scales_g", align_bytes=64)
+        grouped = [keep.tile([P, S, 4], BF16, name=f"grouped{s}", align_bytes=64) for s in range(NPASS)]
+
+        g_first = [keep.tile([P, 4, cn], F32, name=f"g_first{c0}") for c0, cn in CUTS]
+
+        def look_up(dst, s, t, c0, cn):
+            nc.vector.tensor_tensor(
+                dst, dy[s][t][:].indirect(offs_t[:, c0 // 16 : (c0 + cn) // 16]), gate_t[:, c0 : c0 + cn], MULT
+            )
+
+        def interleave(s, src, c0, cn):
+            nc.scalar.copy(
+                out=grouped[s][:, c0 : c0 + cn, :].rearrange("p (c i) t -> p c t i", i=4),
+                in_=src.rearrange("p t (c i) -> p c t i", i=4),
+            )
+
+        def gather_second(c0, cn):
+            g4 = ring2.tile([P, 4, cn], F32, name="g4")
+            for t in range(4):
+                look_up(g4[:, t, :], 1, t, c0, cn)
+            return g4
+
+        def quantize_g(s, c0, cn):
+            nc.vector.quantize_mx(
+                out=codes[:, s, c0 : c0 + cn].bitcast(E4M3X4),
+                scales=scales_g[:, s, c0 : c0 + cn],
+                in_=grouped[s][:, c0 : c0 + cn, :].rearrange("p n t -> p (n t)"),
+            )
+
+        dh = {}
+
+        def first_product(e, h):
+            cols = slice(e * C + h * HALF, e * C + (h + 1) * HALF)
+            dht = psum.tile([P, H], F32, name="dht")
+            for s in range(NPASS):
+                nc.tensor.matmul_mx(
+                    out=dht[:],
+                    lhsT=codes[:, s, cols].bitcast(E4M3X4),
+                    lhsT_scale=scales_g[:, s, cols],
+                    rhs=w2_t[:, e * NPASS + s, :].bitcast(E2M1X4),
+                    rhs_scale=w2s_t[:, e * NPASS + s, :],
+                    start=(s == 0),
+                    stop=(s == NPASS - 1),
+                )
+            turned = ring2.tile([P, 4, P], F32, name="turned")
+            nc.scalar.copy(out=turned[:], in_=dht[:].rearrange("p (q t) -> p t q", t=4))
+            bank = psum.tile([P, 4, HALF], F32, name="bank")
+            for t in range(4):
+                nc.tensor.transpose(bank[:, t, :], turned[:, t, :], ident[:])
+            dh[e, h] = bank
+
+        silu_t = [keep.tile([P, 4, 2 * C], F32, name=f"silu_t{i}") for i in range(2)]
+        nsilu_t = [keep.tile([P, 4, 2 * C], F32, name=f"nsilu_t{i}") for i in range(2)]
+        sig_t = [keep.tile([P, 4, 2 * C], F32, name=f"sig_t{i}") for i in range(2)]
+
+        def nsilu(i):
+            nc.scalar.activation(nsilu_t[i][:], a1_t[i][:], ACT.Silu, scale=-1.0)
+
+        def silu(i):
+            nc.scalar.activation(silu_t[i][:], a1_t[i][:], ACT.Silu)
+
+        def sigmoid(i):
+            nc.scalar.activation(sig_t[i][:], a1_t[i][:], ACT.Sigmoid)
+
+        weighed = {}
+
+        def weigh(e, eng):
+            cols = slice(e % 2 * C, (e % 2 + 1) * C)
+            w = keep.tile([P, 4, C], F32, name="w")
+            eng.tensor_tensor(w[:], sig_t[e // 2][:, :, cols], a3_t[e][:], MULT)
+            weighed[e] = w
+
+        def factor(e):
+            f = nsilu_t[e // 2][:, :, e % 2 * C : (e % 2 + 1) * C]
+            nc.vector.scalar_tensor_tensor(f, f, 1.0, weighed[e][:], SUB, MULT)
+
+        qd = {}
+
+        def products(e, h):
+            da = ring2.tile([P, 2, HALF, 4], BF16, name="da", align_bytes=64)
+            cols = slice(e % 2 * C + h * HALF, e % 2 * C + (h + 1) * HALF)
+            bank = dh[e, h][:].rearrange("p t (c i) -> p c t i", i=4)
+            nc.vector.scalar_tensor_tensor(
+                da[:, 0], nsilu_t[e // 2][:, :, cols].rearrange("p t n -> p n t"), -1.0, dh[e, h][:].rearrange("p t n -> p n t"), MULT, MULT
+            )
+            nc.vector.tensor_tensor(
+                da[:, 1].rearrange("p (c i) t -> p c t i", i=4), bank, silu_t[e // 2][:, :, cols].rearrange("p t (c i) -> p c t i", i=4), MULT
+            )
+            qd[e, h] = da
+
+        def second(e, h):
+            dc = ring3.tile([P, 2, HALF], U32, name="dc", align_bytes=64)
+            ds = ring3.tile([P, 2, HALF], U8, name="ds", align_bytes=64)
+            nc.vector.quantize_mx(
+                out=dc[:].rearrange("p j n -> p (j n)").bitcast(E4M3X4),
+                scales=ds[:].rearrange("p j n -> p (j n)"),
+                in_=qd[e, h][:].rearrange("p j n t -> p (j n t)"),
+            )
+            groups = ((0, 1), (1, 2), (3, 3)) if (e, h) == (E - 1, 1) else ((0, 3), (3, 3))
+            for i, (k0, kn) in enumerate(groups):
+                acc = psum.tile([P, kn, HALF], F32, name=f"acc{i % 2}")
+                for k in range(kn):
+                    kt = k0 + k
+                    for j in range(2):
+                        nc.tensor.matmul_mx(
+                            out=acc[:, k, :],
+                            lhsT=w13_t[j][:, e, 2 * P * kt : 2 * P * (kt + 1)].bitcast(E2M1X4),
+                            lhsT_scale=w13s_t[j][:, e, P * kt : P * (kt + 1)],
+                            rhs=dc[:, j, :].bitcast(E4M3X4),
+                            rhs_scale=ds[:, j, :],
+                            start=(j == 0),
+                            stop=(j == 1),
+                        )
+                slots = slice(e * C + h * HALF, e * C + (h + 1) * HALF)
+                nc.scalar.copy(out=dx_t[:, k0 : k0 + kn, slots], in_=acc[:])
+
+        def combine(kt, c0, cn, eng):
+            cols = slice(c0 // 16, (c0 + cn) // 16)
+            r1 = ring2.tile([P, cn], F32, name="r1")
+            nc.vector.tensor_copy(r1[:], dx_t[:, kt, :].indirect(pos1_t[:, cols]))
+            r2 = ring2.tile([P, cn], F32, name="r2")
+            nc.vector.tensor_copy(r2[:], dx_t[:, kt, :].indirect(pos2_t[:, cols]))
+            o = ring2.tile([P, cn], F32, name="o")
+            eng.tensor_tensor(o[:], r1[:], r2[:], ADD)
+            nc.sync.dma_start(out=out[kt * P : (kt + 1) * P, c0 : c0 + cn], in_=o[:])
+
+        for t in range(4):
+            for i, (c0, cn) in enumerate(CUTS):
+                look_up(g_first[i][:, t, :], 0, t, c0, cn)
+
+        def first_half(i):
+            c0, cn = CUTS[i]
+            interleave(0, g_first[i][:], c0, cn)
+
+        nsilu(0)
+        first_half(0)
+        silu(0)
+        first_half(1)
+        g4 = gather_second(*CUTS[0])
+        interleave(1, g4[:], *CUTS[0])
+        quantize_g(0, 0, 256)
+        nsilu(1)
+        silu(1)
+        sigmoid(0)
+        g4 = gather_second(*CUTS[1])
+        quantize_g(1, 0, 256)
+        first_product(0, 0)
+        interleave(1, g4[:], *CUTS[1])
+        first_product(0, 1)
+        quantize_g(0, 256, 256)
+        first_half(2)
+        weigh(0, nc.vector)
+        factor(0)
+        g4 = gather_second(*CUTS[2])
+        quantize_g(1, 256, 256)
+        interleave(1, g4[:], *CUTS[2])
+        sigmoid(1)
+        quantize_g(0, 512, 512)
+        dx_t = keep.tile([P, KT, S], F32, name="dx_t")
+        for e in range(E):
+            if e > 0:
+                weigh(e, nc.gpsimd)
+                factor(e)
+            if e == 1:
+                quantize_g(1, 512, 512)
+            products(e, 0)
+            if e + 1 < E:
+                first_product(e + 1, 0)
+            if e + 1 == E:
+                second(e, 0)
+            products(e, 1)
+            if e + 1 < E:
+                second(e, 0)
+                first_product(e + 1, 1)
+            second(e, 1)
+        for kt in range(KT - 1):
+            combine(kt, 0, T, nc.gpsimd)
+        combine(KT - 1, 0, T // 2, nc.vector)
+        combine(KT - 1, T // 2, T // 2, nc.vector)

@@ -228,16 +228,19 @@ def tile_moe_bdx_glu_silu_kernel(
                             stop=(j == 1),
                         )
                 slots = slice(e * C + h * HALF, e * C + (h + 1) * HALF)
-                nc.scalar.copy(out=dx_t[:, k0 : k0 + kn, slots], in_=acc[:])
+                for k in range(kn):
+                    nc.scalar.copy(out=dx_t[k0 + k][:, slots], in_=acc[:, k, :])
 
-        def combine(kt, c0, cn, eng):
-            cols = slice(c0 // 16, (c0 + cn) // 16)
-            r1 = ring2.tile([P, cn], F32, name="r1")
-            nc.vector.tensor_copy(r1[:], dx_t[:, kt, :].indirect(pos1_t[:, cols]))
-            r2 = ring2.tile([P, cn], F32, name="r2")
-            nc.vector.tensor_copy(r2[:], dx_t[:, kt, :].indirect(pos2_t[:, cols]))
-            o = ring2.tile([P, cn], F32, name="o")
-            eng.tensor_tensor(o[:], r1[:], r2[:], ADD)
+        firsts = {}
+
+        def fetch_first(kt):
+            r1 = ring3.tile([P, T], F32, name="r1")
+            nc.vector.tensor_copy(r1[:], dx_t[kt][:].indirect(pos1_t[:]))
+            firsts[kt] = r1
+
+        def add_second(kt, c0, cn):
+            o = ring3.tile([P, cn], F32, name="o")
+            nc.vector.tensor_tensor(o[:], dx_t[kt][:].indirect(pos2_t[:, c0 // 16 : (c0 + cn) // 16]), firsts[kt][:, c0 : c0 + cn], ADD)
             nc.sync.dma_start(out=out[kt * P : (kt + 1) * P, c0 : c0 + cn], in_=o[:])
 
         for t in range(4):
@@ -272,7 +275,7 @@ def tile_moe_bdx_glu_silu_kernel(
         interleave(1, g4[:], *CUTS[2])
         sigmoid(1)
         quantize_g(0, 512, 512)
-        dx_t = keep.tile([P, KT, S], F32, name="dx_t")
+        dx_t = [keep.tile([P, S], F32, name=f"dx_t{kt}") for kt in range(KT)]
         for e in range(E):
             if e > 0:
                 weigh(e, nc.gpsimd)
@@ -289,7 +292,9 @@ def tile_moe_bdx_glu_silu_kernel(
                 second(e, 0)
                 first_product(e + 1, 1)
             second(e, 1)
+        fetch_first(0)
         for kt in range(KT - 1):
-            combine(kt, 0, T, nc.gpsimd)
-        combine(KT - 1, 0, T // 2, nc.vector)
-        combine(KT - 1, T // 2, T // 2, nc.vector)
+            fetch_first(kt + 1)
+            add_second(kt, 0, T)
+        add_second(KT - 1, 0, T // 2)
+        add_second(KT - 1, T // 2, T // 2)

@@ -26,7 +26,8 @@ P = 128
 HALF = 128
 NPASS = N // 512
 KT = K // P
-CUTS = ((0, 256), (256, 384), (640, 384))
+EARLY = 2
+CUTS = ((0, 384), (384, 384), (768, 256))
 
 
 def tile_moe_bdx_glu_silu_kernel(
@@ -38,13 +39,14 @@ def tile_moe_bdx_glu_silu_kernel(
         ring3 = ctx.enter_context(tc.tile_pool(name="ring3", bufs=3))
         ring2 = ctx.enter_context(tc.tile_pool(name="ring2", bufs=2))
         psum = ctx.enter_context(tc.psum_pool(name="psum", bufs=2))
+        psum4 = ctx.enter_context(tc.psum_pool(name="psum4", bufs=4))
 
         offs_t = keep.tile([P, S // 16], U16, name="offs_t")
         pos1_t = keep.tile([P, T // 16], U16, name="pos1_t")
         pos2_t = keep.tile([P, T // 16], U16, name="pos2_t")
         dy = [[keep.tile([P, T], F32, name=f"dy{s}{t}") for t in range(4)] for s in range(NPASS)]
         gate_t = keep.tile([P, S], F32, name="gate_t")
-        a1_t = [keep.tile([P, 4, 2 * C], F32, name=f"a1_t{i}") for i in range(2)]
+        a1_t = keep.tile([P, 4, S], F32, name="a1_t")
         a3_t = [keep.tile([P, 4, C], F32, name=f"a3_t{e}") for e in range(E)]
         w2_t = keep.tile([P, E * NPASS, 2 * H], U8, name="w2_t", align_bytes=64)
         w2s_t = keep.tile([P, E * NPASS, H], U8, name="w2s_t", align_bytes=64)
@@ -76,26 +78,27 @@ def tile_moe_bdx_glu_silu_kernel(
             cols = slice(e * C, (e + 1) * C)
             nc.sync.dma_start(out=dst[e][:], in_=src.rearrange("(p t) n -> p t n", t=4)[:, :, cols])
 
-        def load_a1(i):
-            cols = slice(2 * i * C, 2 * (i + 1) * C)
-            nc.sync.dma_start(out=a1_t[i][:], in_=a1.rearrange("(p t) n -> p t n", t=4)[:, :, cols])
+        def load_a1(t):
+            nc.sync.dma_start(out=a1_t[:, t, :], in_=a1.rearrange("(p t) n -> t p n", t=4)[t])
 
-        def load_gate(e):
-            nc.sync.dma_start(out=gate_t[:, e * C : (e + 1) * C], in_=gate[0:P, e * C : (e + 1) * C])
+        def load_gate(c0, cn):
+            nc.sync.dma_start(out=gate_t[:, c0 : c0 + cn], in_=gate[0:P, c0 : c0 + cn])
 
         nc.vector.memset(dummy[:], 0.0)
-        nc.scalar.activation(dummy[:], dummy[:], ACT.Silu)
+        nc.scalar.activation(dummy[:], dummy[:], ACT.Sigmoid)
 
-        nc.scalar.dma_start(out=gate_t[:, 0:C], in_=gate[0:P, 0:C])
+        nc.scalar.dma_start(out=gate_t[:, 0 : CUTS[0][1]], in_=gate[0:P, 0 : CUTS[0][1]])
         nc.sync.dma_start(offs_t[:], offs)
         load_dy(0, 0)
-        for e in range(1, E):
-            load_gate(e)
-        load_dy(0, 1)
+        for c0, cn in CUTS[1:]:
+            load_gate(c0, cn)
         load_a1(0)
-        load_dy(0, 2)
-        load_dy(0, 3)
+        load_dy(0, 1)
         load_a1(1)
+        load_dy(0, 2)
+        load_a1(2)
+        load_a1(3)
+        load_dy(0, 3)
         for t in range(4):
             load_dy(1, t)
         load_w2(0)
@@ -160,76 +163,82 @@ def tile_moe_bdx_glu_silu_kernel(
                 )
             turned = ring2.tile([P, 4, P], F32, name="turned")
             nc.scalar.copy(out=turned[:], in_=dht[:].rearrange("p (q t) -> p t q", t=4))
-            bank = psum.tile([P, 4, HALF], F32, name="bank")
+            bank = psum4.tile([P, 4, HALF], F32, name="bank")
             for t in range(4):
                 nc.tensor.transpose(bank[:, t, :], turned[:, t, :], ident[:])
             dh[e, h] = bank
 
-        silu_t = [keep.tile([P, 4, 2 * C], F32, name=f"silu_t{i}") for i in range(2)]
-        nsilu_t = [keep.tile([P, 4, 2 * C], F32, name=f"nsilu_t{i}") for i in range(2)]
-        sig_t = [keep.tile([P, 4, 2 * C], F32, name=f"sig_t{i}") for i in range(2)]
+        sig_t = keep.tile([P, 4, S], F32, name="sig_t")
 
-        def nsilu(i):
-            nc.scalar.activation(nsilu_t[i][:], a1_t[i][:], ACT.Silu, scale=-1.0)
+        def sigmoid(t):
+            nc.scalar.activation(sig_t[:, t, :], a1_t[:, t, :], ACT.Sigmoid)
 
-        def silu(i):
-            nc.scalar.activation(silu_t[i][:], a1_t[i][:], ACT.Silu)
+        factors = {}
 
-        def sigmoid(i):
-            nc.scalar.activation(sig_t[i][:], a1_t[i][:], ACT.Sigmoid)
+        def nsilu(e):
+            f = ring3.tile([P, 4, C], F32, name="f")
+            nc.scalar.activation(f[:], a1_t[:, :, e * C : (e + 1) * C], ACT.Silu, scale=-1.0)
+            factors[e] = f
+
+        def silu(e):
+            v = a1_t[:, :, e * C : (e + 1) * C]
+            nc.scalar.activation(v, v, ACT.Silu)
 
         weighed = {}
 
         def weigh(e, eng):
-            cols = slice(e % 2 * C, (e % 2 + 1) * C)
             w = keep.tile([P, 4, C], F32, name="w")
-            eng.tensor_tensor(w[:], sig_t[e // 2][:, :, cols], a3_t[e][:], MULT)
+            eng.tensor_tensor(w[:], sig_t[:, :, e * C : (e + 1) * C], a3_t[e][:], MULT)
             weighed[e] = w
 
         def factor(e):
-            f = nsilu_t[e // 2][:, :, e % 2 * C : (e % 2 + 1) * C]
+            f = factors[e][:]
             nc.vector.scalar_tensor_tensor(f, f, 1.0, weighed[e][:], SUB, MULT)
 
         qd = {}
 
         def products(e, h):
-            da = ring2.tile([P, 2, HALF, 4], BF16, name="da", align_bytes=64)
-            cols = slice(e % 2 * C + h * HALF, e % 2 * C + (h + 1) * HALF)
+            da = ring3.tile([P, 2, HALF, 4], BF16, name="da", align_bytes=64)
+            cols = slice(e * C + h * HALF, e * C + (h + 1) * HALF)
             bank = dh[e, h][:].rearrange("p t (c i) -> p c t i", i=4)
-            nc.vector.scalar_tensor_tensor(
-                da[:, 0], nsilu_t[e // 2][:, :, cols].rearrange("p t n -> p n t"), -1.0, dh[e, h][:].rearrange("p t n -> p n t"), MULT, MULT
-            )
             nc.vector.tensor_tensor(
-                da[:, 1].rearrange("p (c i) t -> p c t i", i=4), bank, silu_t[e // 2][:, :, cols].rearrange("p t (c i) -> p c t i", i=4), MULT
+                da[:, 1].rearrange("p (c i) t -> p c t i", i=4), bank, a1_t[:, :, cols].rearrange("p t (c i) -> p c t i", i=4), MULT
+            )
+            nc.vector.scalar_tensor_tensor(
+                da[:, 0], factors[e][:, :, h * HALF : (h + 1) * HALF].rearrange("p t n -> p n t"), -1.0, dh[e, h][:].rearrange("p t n -> p n t"), MULT, MULT
             )
             qd[e, h] = da
 
-        def second(e, h):
-            dc = ring3.tile([P, 2, HALF], U32, name="dc", align_bytes=64)
-            ds = ring3.tile([P, 2, HALF], U8, name="ds", align_bytes=64)
+        coded = {}
+
+        def quantize_da(e, h):
+            dc = keep.tile([P, 2, HALF], U32, name=f"dc{e}{h}", align_bytes=64)
+            ds = keep.tile([P, 2, HALF], U8, name=f"ds{e}{h}", align_bytes=64)
             nc.vector.quantize_mx(
                 out=dc[:].rearrange("p j n -> p (j n)").bitcast(E4M3X4),
                 scales=ds[:].rearrange("p j n -> p (j n)"),
                 in_=qd[e, h][:].rearrange("p j n t -> p (j n t)"),
             )
-            groups = ((0, 1), (1, 2), (3, 3)) if (e, h) == (E - 1, 1) else ((0, 3), (3, 3))
-            for i, (k0, kn) in enumerate(groups):
-                acc = psum.tile([P, kn, HALF], F32, name=f"acc{i % 2}")
-                for k in range(kn):
-                    kt = k0 + k
-                    for j in range(2):
-                        nc.tensor.matmul_mx(
-                            out=acc[:, k, :],
-                            lhsT=w13_t[j][:, e, 2 * P * kt : 2 * P * (kt + 1)].bitcast(E2M1X4),
-                            lhsT_scale=w13s_t[j][:, e, P * kt : P * (kt + 1)],
-                            rhs=dc[:, j, :].bitcast(E4M3X4),
-                            rhs_scale=ds[:, j, :],
-                            start=(j == 0),
-                            stop=(j == 1),
-                        )
-                slots = slice(e * C + h * HALF, e * C + (h + 1) * HALF)
-                for k in range(kn):
-                    nc.scalar.copy(out=dx_t[k0 + k][:, slots], in_=acc[:, k, :])
+            coded[e, h] = dc, ds
+
+        def second_group(dst, e, h, kt):
+            dc, ds = coded[e, h]
+            for j in range(2):
+                nc.tensor.matmul_mx(
+                    out=dst,
+                    lhsT=w13_t[j][:, e, 2 * P * kt : 2 * P * (kt + 1)].bitcast(E2M1X4),
+                    lhsT_scale=w13s_t[j][:, e, P * kt : P * (kt + 1)],
+                    rhs=dc[:, j, :].bitcast(E4M3X4),
+                    rhs_scale=ds[:, j, :],
+                    start=(j == 0),
+                    stop=(j == 1),
+                )
+
+        def second(pool, tag, kt, first, count):
+            acc = pool.tile([P, count, HALF], F32, name=tag)
+            for i in range(count):
+                second_group(acc[:, i, :], (first + i) // 2, (first + i) % 2, kt)
+            nc.scalar.copy(out=dx_t[kt][:, first * HALF : (first + count) * HALF], in_=acc[:].rearrange("p i n -> p (i n)"))
 
         firsts = {}
 
@@ -251,47 +260,58 @@ def tile_moe_bdx_glu_silu_kernel(
             c0, cn = CUTS[i]
             interleave(0, g_first[i][:], c0, cn)
 
+        for t in range(4):
+            sigmoid(t)
         nsilu(0)
-        first_half(0)
         silu(0)
-        first_half(1)
+        first_half(0)
         g4 = gather_second(*CUTS[0])
         interleave(1, g4[:], *CUTS[0])
-        quantize_g(0, 0, 256)
-        nsilu(1)
-        silu(1)
-        sigmoid(0)
+        first_half(1)
         g4 = gather_second(*CUTS[1])
+        quantize_g(0, 0, 256)
         quantize_g(1, 0, 256)
-        first_product(0, 0)
+        nsilu(1)
         interleave(1, g4[:], *CUTS[1])
-        first_product(0, 1)
-        quantize_g(0, 256, 256)
-        first_half(2)
-        weigh(0, nc.vector)
-        factor(0)
         g4 = gather_second(*CUTS[2])
-        quantize_g(1, 256, 256)
-        interleave(1, g4[:], *CUTS[2])
-        sigmoid(1)
-        quantize_g(0, 512, 512)
+        first_product(0, 0)
+        first_product(0, 1)
+        weigh(0, nc.vector)
+        quantize_g(0, 256, 512)
+        quantize_g(1, 256, 512)
+        factor(0)
+        silu(1)
         dx_t = [keep.tile([P, S], F32, name=f"dx_t{kt}") for kt in range(KT)]
         for e in range(E):
-            if e > 0:
-                weigh(e, nc.gpsimd)
-                factor(e)
-            if e == 1:
-                quantize_g(1, 512, 512)
-            products(e, 0)
             if e + 1 < E:
+                weigh(e + 1, nc.gpsimd)
                 first_product(e + 1, 0)
-            if e + 1 == E:
-                second(e, 0)
-            products(e, 1)
-            if e + 1 < E:
-                second(e, 0)
                 first_product(e + 1, 1)
-            second(e, 1)
+            if e == 0:
+                first_half(2)
+                interleave(1, g4[:], *CUTS[2])
+            if e + 2 < E:
+                nsilu(e + 2)
+                silu(e + 2)
+            if e == E - 1:
+                for kt in range(EARLY):
+                    second(psum, "acc", kt, 0, 4)
+            products(e, 0)
+            products(e, 1)
+            quantize_da(e, 0)
+            quantize_da(e, 1)
+            if e == 0:
+                quantize_g(0, 768, 256)
+                quantize_g(1, 768, 256)
+            if e + 1 < E:
+                factor(e + 1)
+        for kt in range(EARLY):
+            second(psum, "acc", kt, 4, 3)
+        for kt in range(EARLY):
+            second(psum4, "bank", kt, 7, 1)
+        for kt in range(EARLY, KT):
+            second(psum, "dht", kt, 0, 4)
+            second(psum4, "bank", kt, 4, 4)
         fetch_first(0)
         for kt in range(KT - 1):
             fetch_first(kt + 1)

@@ -28,6 +28,7 @@ NPASS = N // 512
 KT = K // P
 EARLY = 2
 CUTS = ((0, 384), (384, 384), (768, 256))
+OPENING = ((0, 128), (128, 448), (576, 448))
 
 
 def tile_moe_bdx_glu_silu_kernel(
@@ -87,18 +88,18 @@ def tile_moe_bdx_glu_silu_kernel(
         nc.vector.memset(dummy[:], 0.0)
         nc.scalar.activation(dummy[:], dummy[:], ACT.Sigmoid)
 
-        nc.scalar.dma_start(out=gate_t[:, 0 : CUTS[0][1]], in_=gate[0:P, 0 : CUTS[0][1]])
+        nc.scalar.dma_start(out=gate_t[:, 0 : OPENING[0][1]], in_=gate[0:P, 0 : OPENING[0][1]])
         nc.sync.dma_start(offs_t[:], offs)
         load_dy(0, 0)
-        for c0, cn in CUTS[1:]:
+        for c0, cn in OPENING[1:]:
             load_gate(c0, cn)
-        load_a1(0)
         load_dy(0, 1)
+        load_a1(0)
         load_a1(1)
         load_dy(0, 2)
         load_a1(2)
-        load_a1(3)
         load_dy(0, 3)
+        load_a1(3)
         for t in range(4):
             load_dy(1, t)
         load_w2(0)
@@ -120,7 +121,7 @@ def tile_moe_bdx_glu_silu_kernel(
         scales_g = keep.tile([P, NPASS, S], U8, name="scales_g", align_bytes=64)
         grouped = [keep.tile([P, S, 4], BF16, name=f"grouped{s}", align_bytes=64) for s in range(NPASS)]
 
-        g_first = [keep.tile([P, 4, cn], F32, name=f"g_first{c0}") for c0, cn in CUTS]
+        g_first = keep.tile([P, 4, S], F32, name="g_first")
 
         def look_up(dst, s, t, c0, cn):
             nc.vector.tensor_tensor(
@@ -173,40 +174,43 @@ def tile_moe_bdx_glu_silu_kernel(
         def sigmoid(t):
             nc.scalar.activation(sig_t[:, t, :], a1_t[:, t, :], ACT.Sigmoid)
 
-        factors = {}
+        nsilu_t = [keep.tile([P, 4, C], F32, name=f"nsilu_t{e}", align_bytes=64) for e in range(E)]
+        weighed = [keep.tile([P, 4, C], F32, name="weighed0", align_bytes=64)] + nsilu_t[: E - 1]
 
         def nsilu(e):
-            f = ring3.tile([P, 4, C], F32, name="f")
-            nc.scalar.activation(f[:], a1_t[:, :, e * C : (e + 1) * C], ACT.Silu, scale=-1.0)
-            factors[e] = f
+            nc.scalar.activation(nsilu_t[e][:], a1_t[:, :, e * C : (e + 1) * C], ACT.Silu, scale=-1.0)
 
         def silu(e):
             v = a1_t[:, :, e * C : (e + 1) * C]
             nc.scalar.activation(v, v, ACT.Silu)
 
-        weighed = {}
+        def weigh(e):
+            if e == 0:
+                nc.vector.scalar_tensor_tensor(weighed[e][:], sig_t[:, :, 0:C], -1.0, a3_t[e][:], MULT, MULT)
+            else:
+                nc.gpsimd.tensor_tensor(weighed[e][:], sig_t[:, :, e * C : (e + 1) * C], a3_t[e][:], MULT)
 
-        def weigh(e, eng):
-            w = keep.tile([P, 4, C], F32, name="w")
-            eng.tensor_tensor(w[:], sig_t[:, :, e * C : (e + 1) * C], a3_t[e][:], MULT)
-            weighed[e] = w
+        factors = {}
 
         def factor(e):
-            f = factors[e][:]
-            nc.vector.scalar_tensor_tensor(f, f, 1.0, weighed[e][:], SUB, MULT)
+            f = ring2.tile([P, 4, C], F32, name="f")
+            nc.vector.scalar_tensor_tensor(f[:], nsilu_t[e][:], 1.0, weighed[e][:], SUB, MULT)
+            factors[e] = f
 
         qd = {}
 
         def products(e, h):
-            da = ring3.tile([P, 2, HALF, 4], BF16, name="da", align_bytes=64)
+            da = weighed[e][:].rearrange("p t n -> p (t n)").bitcast(BF16).rearrange("p (h j n t) -> p h j n t", h=2, j=2, t=4)[:, h]
             cols = slice(e * C + h * HALF, e * C + (h + 1) * HALF)
             bank = dh[e, h][:].rearrange("p t (c i) -> p c t i", i=4)
             nc.vector.tensor_tensor(
                 da[:, 1].rearrange("p (c i) t -> p c t i", i=4), bank, a1_t[:, :, cols].rearrange("p t (c i) -> p c t i", i=4), MULT
             )
-            nc.vector.scalar_tensor_tensor(
-                da[:, 0], factors[e][:, :, h * HALF : (h + 1) * HALF].rearrange("p t n -> p n t"), -1.0, dh[e, h][:].rearrange("p t n -> p n t"), MULT, MULT
-            )
+            f = factors[e][:, :, h * HALF : (h + 1) * HALF]
+            if e == 0:
+                nc.vector.tensor_tensor(da[:, 0].rearrange("p (c i) t -> p c t i", i=4), bank, f.rearrange("p t (c i) -> p c t i", i=4), MULT)
+            else:
+                nc.vector.scalar_tensor_tensor(da[:, 0], f.rearrange("p t n -> p n t"), -1.0, dh[e, h][:].rearrange("p t n -> p n t"), MULT, MULT)
             qd[e, h] = da
 
         coded = {}
@@ -217,7 +221,7 @@ def tile_moe_bdx_glu_silu_kernel(
             nc.vector.quantize_mx(
                 out=dc[:].rearrange("p j n -> p (j n)").bitcast(E4M3X4),
                 scales=ds[:].rearrange("p j n -> p (j n)"),
-                in_=qd[e, h][:].rearrange("p j n t -> p (j n t)"),
+                in_=qd[e, h].rearrange("p j n t -> p (j n t)"),
             )
             coded[e, h] = dc, ds
 
@@ -234,11 +238,11 @@ def tile_moe_bdx_glu_silu_kernel(
                     stop=(j == 1),
                 )
 
-        def second(pool, tag, kt, first, count):
+        def second(pool, tag, kt, first, count, copy=nc.scalar.copy):
             acc = pool.tile([P, count, HALF], F32, name=tag)
-            for i in range(count):
+            for i in reversed(range(count)):
                 second_group(acc[:, i, :], (first + i) // 2, (first + i) % 2, kt)
-            nc.scalar.copy(out=dx_t[kt][:, first * HALF : (first + count) * HALF], in_=acc[:].rearrange("p i n -> p (i n)"))
+            copy(out=dx_t[kt][:, first * HALF : (first + count) * HALF], in_=acc[:].rearrange("p i n -> p (i n)"))
 
         firsts = {}
 
@@ -253,47 +257,43 @@ def tile_moe_bdx_glu_silu_kernel(
             nc.sync.dma_start(out=out[kt * P : (kt + 1) * P, c0 : c0 + cn], in_=o[:])
 
         for t in range(4):
-            for i, (c0, cn) in enumerate(CUTS):
-                look_up(g_first[i][:, t, :], 0, t, c0, cn)
+            for c0, cn in CUTS if t else OPENING:
+                look_up(g_first[:, t, c0 : c0 + cn], 0, t, c0, cn)
 
         def first_half(i):
             c0, cn = CUTS[i]
-            interleave(0, g_first[i][:], c0, cn)
+            interleave(0, g_first[:, :, c0 : c0 + cn], c0, cn)
 
         for t in range(4):
             sigmoid(t)
-        nsilu(0)
-        silu(0)
         first_half(0)
+        first_half(1)
+        first_half(2)
         g4 = gather_second(*CUTS[0])
         interleave(1, g4[:], *CUTS[0])
-        first_half(1)
+        nsilu(0)
         g4 = gather_second(*CUTS[1])
         quantize_g(0, 0, 256)
         quantize_g(1, 0, 256)
-        nsilu(1)
         interleave(1, g4[:], *CUTS[1])
         g4 = gather_second(*CUTS[2])
         first_product(0, 0)
         first_product(0, 1)
-        weigh(0, nc.vector)
+        silu(0)
+        interleave(1, g4[:], *CUTS[2])
+        weigh(0)
         quantize_g(0, 256, 512)
         quantize_g(1, 256, 512)
         factor(0)
-        silu(1)
         dx_t = [keep.tile([P, S], F32, name=f"dx_t{kt}") for kt in range(KT)]
         for e in range(E):
             if e + 1 < E:
-                weigh(e + 1, nc.gpsimd)
+                nsilu(e + 1)
+                weigh(e + 1)
                 first_product(e + 1, 0)
                 first_product(e + 1, 1)
-            if e == 0:
-                first_half(2)
-                interleave(1, g4[:], *CUTS[2])
-            if e + 2 < E:
-                nsilu(e + 2)
-                silu(e + 2)
-            if e == E - 1:
+                silu(e + 1)
+            if e == E - 2:
                 for kt in range(EARLY):
                     second(psum, "acc", kt, 0, 4)
             products(e, 0)
@@ -305,16 +305,18 @@ def tile_moe_bdx_glu_silu_kernel(
                 quantize_g(1, 768, 256)
             if e + 1 < E:
                 factor(e + 1)
-        for kt in range(EARLY):
-            second(psum, "acc", kt, 4, 3)
-        for kt in range(EARLY):
-            second(psum4, "bank", kt, 7, 1)
+            if e == E - 2:
+                for kt in range(EARLY):
+                    second(psum, "acc", kt, 4, 2)
+        second(psum, "dht", 0, 6, 1)
+        second(psum, "dht", 0, 7, 1, nc.vector.tensor_copy)
+        second(psum4, "bank", 1, 6, 2)
         for kt in range(EARLY, KT):
-            second(psum, "dht", kt, 0, 4)
+            second(psum, "acc", kt, 0, 4)
             second(psum4, "bank", kt, 4, 4)
         fetch_first(0)
         for kt in range(KT - 1):
             fetch_first(kt + 1)
             add_second(kt, 0, T)
-        add_second(KT - 1, 0, T // 2)
-        add_second(KT - 1, T // 2, T // 2)
+        add_second(KT - 1, 0, T - P)
+        add_second(KT - 1, T - P, P)

@@ -89,8 +89,8 @@ def tile_moe_bdx_glu_silu_kernel(
         nc.scalar.activation(dummy[:], dummy[:], ACT.Sigmoid)
 
         nc.scalar.dma_start(out=gate_t[:, 0 : OPENING[0][1]], in_=gate[0:P, 0 : OPENING[0][1]])
-        nc.sync.dma_start(offs_t[:], offs)
         load_dy(0, 0)
+        nc.sync.dma_start(offs_t[:], offs)
         for c0, cn in OPENING[1:]:
             load_gate(c0, cn)
         load_dy(0, 1)
@@ -177,12 +177,13 @@ def tile_moe_bdx_glu_silu_kernel(
         nsilu_t = [keep.tile([P, 4, C], F32, name=f"nsilu_t{e}", align_bytes=64) for e in range(E)]
         weighed = [keep.tile([P, 4, C], F32, name="weighed0", align_bytes=64)] + nsilu_t[: E - 1]
 
+        silu_t = g_first[:].rearrange("p t n -> p (t n)").rearrange("p (e t n) -> p e t n", e=E, t=4)
+
         def nsilu(e):
             nc.scalar.activation(nsilu_t[e][:], a1_t[:, :, e * C : (e + 1) * C], ACT.Silu, scale=-1.0)
 
         def silu(e):
-            v = a1_t[:, :, e * C : (e + 1) * C]
-            nc.scalar.activation(v, v, ACT.Silu)
+            nc.scalar.activation(silu_t[:, e], a1_t[:, :, e * C : (e + 1) * C], ACT.Silu)
 
         def weigh(e):
             if e == 0:
@@ -201,14 +202,13 @@ def tile_moe_bdx_glu_silu_kernel(
 
         def products(e, h):
             da = weighed[e][:].rearrange("p t n -> p (t n)").bitcast(BF16).rearrange("p (h j n t) -> p h j n t", h=2, j=2, t=4)[:, h]
-            cols = slice(e * C + h * HALF, e * C + (h + 1) * HALF)
-            bank = dh[e, h][:].rearrange("p t (c i) -> p c t i", i=4)
+            bank = dh[e, h][:].rearrange("p t (c i) -> p c t i", i=2)
             nc.vector.tensor_tensor(
-                da[:, 1].rearrange("p (c i) t -> p c t i", i=4), bank, a1_t[:, :, cols].rearrange("p t (c i) -> p c t i", i=4), MULT
+                da[:, 1].rearrange("p (c i) t -> p c t i", i=2), bank, silu_t[:, e, :, h * HALF : (h + 1) * HALF].rearrange("p t (c i) -> p c t i", i=2), MULT
             )
             f = factors[e][:, :, h * HALF : (h + 1) * HALF]
             if e == 0:
-                nc.vector.tensor_tensor(da[:, 0].rearrange("p (c i) t -> p c t i", i=4), bank, f.rearrange("p t (c i) -> p c t i", i=4), MULT)
+                nc.vector.tensor_tensor(da[:, 0].rearrange("p (c i) t -> p c t i", i=2), bank, f.rearrange("p t (c i) -> p c t i", i=2), MULT)
             else:
                 nc.vector.scalar_tensor_tensor(da[:, 0], f.rearrange("p t n -> p n t"), -1.0, dh[e, h][:].rearrange("p t n -> p n t"), MULT, MULT)
             qd[e, h] = da
@@ -282,9 +282,10 @@ def tile_moe_bdx_glu_silu_kernel(
         silu(0)
         interleave(1, g4[:], *CUTS[2])
         weigh(0)
-        quantize_g(0, 256, 512)
+        quantize_g(0, 256, 256)
         quantize_g(1, 256, 512)
         factor(0)
+        quantize_g(0, 512, 512)
         dx_t = [keep.tile([P, S], F32, name=f"dx_t{kt}") for kt in range(KT)]
         for e in range(E):
             if e + 1 < E:
@@ -299,12 +300,11 @@ def tile_moe_bdx_glu_silu_kernel(
             products(e, 0)
             products(e, 1)
             quantize_da(e, 0)
-            quantize_da(e, 1)
             if e == 0:
-                quantize_g(0, 768, 256)
                 quantize_g(1, 768, 256)
             if e + 1 < E:
                 factor(e + 1)
+            quantize_da(e, 1)
             if e == E - 2:
                 for kt in range(EARLY):
                     second(psum, "acc", kt, 4, 2)

@@ -202,13 +202,13 @@ def tile_moe_bdx_glu_silu_kernel(
 
         def products(e, h):
             da = weighed[e][:].rearrange("p t n -> p (t n)").bitcast(BF16).rearrange("p (h j n t) -> p h j n t", h=2, j=2, t=4)[:, h]
-            bank = dh[e, h][:].rearrange("p t (c i) -> p c t i", i=2)
+            bank = dh[e, h][:].rearrange("p t (c i) -> p c t i", i=4)
             nc.vector.tensor_tensor(
-                da[:, 1].rearrange("p (c i) t -> p c t i", i=2), bank, silu_t[:, e, :, h * HALF : (h + 1) * HALF].rearrange("p t (c i) -> p c t i", i=2), MULT
+                da[:, 1].rearrange("p (c i) t -> p c t i", i=4), bank, silu_t[:, e, :, h * HALF : (h + 1) * HALF].rearrange("p t (c i) -> p c t i", i=4), MULT
             )
             f = factors[e][:, :, h * HALF : (h + 1) * HALF]
             if e == 0:
-                nc.vector.tensor_tensor(da[:, 0].rearrange("p (c i) t -> p c t i", i=2), bank, f.rearrange("p t (c i) -> p c t i", i=2), MULT)
+                nc.vector.tensor_tensor(da[:, 0].rearrange("p (c i) t -> p c t i", i=4), bank, f.rearrange("p t (c i) -> p c t i", i=4), MULT)
             else:
                 nc.vector.scalar_tensor_tensor(da[:, 0], f.rearrange("p t n -> p n t"), -1.0, dh[e, h][:].rearrange("p t n -> p n t"), MULT, MULT)
             qd[e, h] = da

@@ -169,10 +169,10 @@ def tile_moe_bdx_glu_silu_kernel(
                 nc.tensor.transpose(bank[:, t, :], turned[:, t, :], ident[:])
             dh[e, h] = bank
 
-        sig_t = keep.tile([P, 4, S], F32, name="sig_t")
+        sig_t = keep.tile([P, E, 4, C], F32, name="sig_t")
 
         def sigmoid(t):
-            nc.scalar.activation(sig_t[:, t, :], a1_t[:, t, :], ACT.Sigmoid)
+            nc.scalar.activation(sig_t[:, :, t, :], a1_t[:, t, :].rearrange("p (e n) -> p e n", e=E), ACT.Sigmoid)
 
         nsilu_t = [keep.tile([P, 4, C], F32, name=f"nsilu_t{e}", align_bytes=64) for e in range(E)]
         weighed = [keep.tile([P, 4, C], F32, name="weighed0", align_bytes=64)] + nsilu_t[: E - 1]
@@ -187,9 +187,9 @@ def tile_moe_bdx_glu_silu_kernel(
 
         def weigh(e):
             if e == 0:
-                nc.vector.scalar_tensor_tensor(weighed[e][:], sig_t[:, :, 0:C], -1.0, a3_t[e][:], MULT, MULT)
+                nc.vector.scalar_tensor_tensor(weighed[e][:], sig_t[:, e], -1.0, a3_t[e][:], MULT, MULT)
             else:
-                nc.gpsimd.tensor_tensor(weighed[e][:], sig_t[:, :, e * C : (e + 1) * C], a3_t[e][:], MULT)
+                nc.gpsimd.tensor_tensor(weighed[e][:], sig_t[:, e], a3_t[e][:], MULT)
 
         factors = {}
 
@@ -204,11 +204,11 @@ def tile_moe_bdx_glu_silu_kernel(
             da = weighed[e][:].rearrange("p t n -> p (t n)").bitcast(BF16).rearrange("p (h j n t) -> p h j n t", h=2, j=2, t=4)[:, h]
             bank = dh[e, h][:].rearrange("p t (c i) -> p c t i", i=4)
             nc.vector.tensor_tensor(
-                da[:, 1].rearrange("p (c i) t -> p c t i", i=4), bank, silu_t[:, e, :, h * HALF : (h + 1) * HALF].rearrange("p t (c i) -> p c t i", i=4), MULT
+                da[:, 1].rearrange("p (c i) t -> p c t i", i=4), silu_t[:, e, :, h * HALF : (h + 1) * HALF].rearrange("p t (c i) -> p c t i", i=4), bank, MULT
             )
             f = factors[e][:, :, h * HALF : (h + 1) * HALF]
             if e == 0:
-                nc.vector.tensor_tensor(da[:, 0].rearrange("p (c i) t -> p c t i", i=4), bank, f.rearrange("p t (c i) -> p c t i", i=4), MULT)
+                nc.vector.tensor_tensor(da[:, 0].rearrange("p (c i) t -> p c t i", i=4), f.rearrange("p t (c i) -> p c t i", i=4), bank, MULT)
             else:
                 nc.vector.scalar_tensor_tensor(da[:, 0], f.rearrange("p t n -> p n t"), -1.0, dh[e, h][:].rearrange("p t n -> p n t"), MULT, MULT)
             qd[e, h] = da

@@ -23,12 +23,15 @@ SUB = mybir.AluOpType.subtract
 ADD = mybir.AluOpType.add
 
 P = 128
+R = 4
 HALF = 128
-NPASS = N // 512
+HALVES = S // HALF
+NPASS = N // (P * R)
 KT = K // P
-EARLY = 2
+RUN = 4
 CUTS = ((0, 384), (384, 384), (768, 256))
 OPENING = ((0, 128), (128, 448), (576, 448))
+EARLY = 2
 
 
 def tile_moe_bdx_glu_silu_kernel(
@@ -39,22 +42,21 @@ def tile_moe_bdx_glu_silu_kernel(
         keep = ctx.enter_context(tc.tile_pool(name="keep", bufs=1))
         ring3 = ctx.enter_context(tc.tile_pool(name="ring3", bufs=3))
         ring2 = ctx.enter_context(tc.tile_pool(name="ring2", bufs=2))
-        psum = ctx.enter_context(tc.psum_pool(name="psum", bufs=2))
+        psum2 = ctx.enter_context(tc.psum_pool(name="psum2", bufs=2))
         psum4 = ctx.enter_context(tc.psum_pool(name="psum4", bufs=4))
 
         offs_t = keep.tile([P, S // 16], U16, name="offs_t")
         pos1_t = keep.tile([P, T // 16], U16, name="pos1_t")
         pos2_t = keep.tile([P, T // 16], U16, name="pos2_t")
-        dy = [[keep.tile([P, T], F32, name=f"dy{s}{t}") for t in range(4)] for s in range(NPASS)]
+        dy = [[keep.tile([P, T], F32, name=f"dy{s}{t}") for t in range(R)] for s in range(NPASS)]
         gate_t = keep.tile([P, S], F32, name="gate_t")
-        a1_t = keep.tile([P, 4, S], F32, name="a1_t")
-        a3_t = [keep.tile([P, 4, C], F32, name=f"a3_t{e}") for e in range(E)]
+        a1_t = keep.tile([P, R, S], F32, name="a1_t")
+        a3_t = [keep.tile([P, R, C], F32, name=f"a3_t{e}") for e in range(E)]
         w2_t = keep.tile([P, E * NPASS, 2 * H], U8, name="w2_t", align_bytes=64)
         w2s_t = keep.tile([P, E * NPASS, H], U8, name="w2s_t", align_bytes=64)
         w13_t = [keep.tile([P, E, 2 * K], U8, name=f"w13_t{j}", align_bytes=64) for j in range(2)]
         w13s_t = [keep.tile([P, E, K], U8, name=f"w13s_t{j}", align_bytes=64) for j in range(2)]
         ident = keep.tile([P, P], F32, name="ident")
-        dummy = keep.tile([P, 1], F32, name="dummy")
 
         nc.gpsimd.memset(w2s_t[:].bitcast(I32), 0)
         nc.gpsimd.memset(w13s_t[0][:].bitcast(I32), 0)
@@ -62,122 +64,118 @@ def tile_moe_bdx_glu_silu_kernel(
         make_identity(nc, ident[:])
 
         def load_dy(s, t):
-            rows = dyT[512 * s : 512 * (s + 1), :].rearrange("(p t) n -> t p n", t=4)
+            rows = dyT[P * R * s : P * R * (s + 1), :].rearrange("(p t) n -> t p n", t=R)
             nc.sync.dma_start(out=dy[s][t][:], in_=rows[t])
+
+        def load_gate(queue, c0, cn):
+            queue.dma_start(out=gate_t[:, c0 : c0 + cn], in_=gate[0:P, c0 : c0 + cn])
+
+        def load_a1(t):
+            nc.sync.dma_start(out=a1_t[:, t, :], in_=a1.rearrange("(p t) n -> t p n", t=R)[t])
+
+        def load_a3(e):
+            nc.sync.dma_start(out=a3_t[e][:], in_=a3.rearrange("(p t) n -> p t n", t=R)[:, :, e * C : (e + 1) * C])
 
         def load_w2(e):
             src = w2_words.bitcast(I32).rearrange("e s p n -> p (e s) n")
-            es = slice(e * NPASS, (e + 1) * NPASS)
-            nc.sync.dma_start(out=w2_t[:, es, :].bitcast(I32), in_=src[:, es, :])
+            passes = slice(e * NPASS, (e + 1) * NPASS)
+            nc.sync.dma_start(out=w2_t[:, passes, :].bitcast(I32), in_=src[:, passes, :])
 
         def load_scales(dst, src):
             view = src.bitcast(I32).rearrange("e s (q r) i -> r q (e s) i", r=4)
             for r in range(4):
                 nc.sync.dma_start(out=dst[:].bitcast(I32)[r : P : 32, :, :], in_=view[r])
 
-        def load_a(dst, src, e):
-            cols = slice(e * C, (e + 1) * C)
-            nc.sync.dma_start(out=dst[e][:], in_=src.rearrange("(p t) n -> p t n", t=4)[:, :, cols])
-
-        def load_a1(t):
-            nc.sync.dma_start(out=a1_t[:, t, :], in_=a1.rearrange("(p t) n -> t p n", t=4)[t])
-
-        def load_gate(c0, cn):
-            nc.sync.dma_start(out=gate_t[:, c0 : c0 + cn], in_=gate[0:P, c0 : c0 + cn])
-
-        nc.vector.memset(dummy[:], 0.0)
-        nc.scalar.activation(dummy[:], dummy[:], ACT.Sigmoid)
-
-        nc.scalar.dma_start(out=gate_t[:, 0 : OPENING[0][1]], in_=gate[0:P, 0 : OPENING[0][1]])
+        load_gate(nc.scalar, *OPENING[0])
         load_dy(0, 0)
         nc.sync.dma_start(offs_t[:], offs)
         for c0, cn in OPENING[1:]:
-            load_gate(c0, cn)
+            load_gate(nc.sync, c0, cn)
         load_dy(0, 1)
         load_a1(0)
-        load_a1(1)
         load_dy(0, 2)
+        load_a1(1)
         load_a1(2)
         load_dy(0, 3)
         load_a1(3)
-        for t in range(4):
+        for t in range(R):
             load_dy(1, t)
         load_w2(0)
         load_scales(w2s_t, w2_scales)
+        load_a3(0)
         load_w2(1)
-        load_a(a3_t, a3, 0)
+        load_a3(1)
         load_w2(2)
         load_w2(3)
-        load_a(a3_t, a3, 1)
+        load_a3(2)
         for j, (words, scales) in enumerate(((w1_words, w1_scales), (w3_words, w3_scales))):
             nc.sync.dma_start(out=w13_t[j][:].bitcast(I32), in_=words.bitcast(I32).rearrange("e s p n -> p (e s) n"))
             load_scales(w13s_t[j], scales)
-        load_a(a3_t, a3, 2)
-        load_a(a3_t, a3, 3)
+        load_a3(3)
         nc.sync.dma_start(pos1_t[:], pos1)
         nc.sync.dma_start(pos2_t[:], pos2)
 
-        codes = keep.tile([P, NPASS, S], U32, name="codes", align_bytes=64)
-        scales_g = keep.tile([P, NPASS, S], U8, name="scales_g", align_bytes=64)
-        grouped = [keep.tile([P, S, 4], BF16, name=f"grouped{s}", align_bytes=64) for s in range(NPASS)]
-
-        g_first = keep.tile([P, 4, S], F32, name="g_first")
+        g_codes = keep.tile([P, NPASS, S], U32, name="g_codes", align_bytes=64)
+        g_scales = keep.tile([P, NPASS, S], U8, name="g_scales", align_bytes=64)
+        g_words = [keep.tile([P, S, R], BF16, name=f"g_words{s}", align_bytes=64) for s in range(NPASS)]
+        g_pass0 = keep.tile([P, R, S], F32, name="g_pass0")
 
         def look_up(dst, s, t, c0, cn):
             nc.vector.tensor_tensor(
                 dst, dy[s][t][:].indirect(offs_t[:, c0 // 16 : (c0 + cn) // 16]), gate_t[:, c0 : c0 + cn], MULT
             )
 
-        def interleave(s, src, c0, cn):
-            nc.scalar.copy(
-                out=grouped[s][:, c0 : c0 + cn, :].rearrange("p (c i) t -> p c t i", i=4),
-                in_=src.rearrange("p t (c i) -> p c t i", i=4),
-            )
+        def look_up_pass1(c0, cn):
+            g_cut = ring2.tile([P, R, cn], F32, name="g_cut")
+            for t in range(R):
+                look_up(g_cut[:, t, :], 1, t, c0, cn)
+            return g_cut
 
-        def gather_second(c0, cn):
-            g4 = ring2.tile([P, 4, cn], F32, name="g4")
-            for t in range(4):
-                look_up(g4[:, t, :], 1, t, c0, cn)
-            return g4
+        def by_runs(slot_major):
+            return slot_major.rearrange("p (c i) t -> p c t i", i=RUN)
+
+        def rows_by_runs(residue_major):
+            return residue_major.rearrange("p t (c i) -> p c t i", i=RUN)
+
+        def interleave(s, src, c0, cn):
+            nc.scalar.copy(out=by_runs(g_words[s][:, c0 : c0 + cn, :]), in_=rows_by_runs(src))
 
         def quantize_g(s, c0, cn):
             nc.vector.quantize_mx(
-                out=codes[:, s, c0 : c0 + cn].bitcast(E4M3X4),
-                scales=scales_g[:, s, c0 : c0 + cn],
-                in_=grouped[s][:, c0 : c0 + cn, :].rearrange("p n t -> p (n t)"),
+                out=g_codes[:, s, c0 : c0 + cn].bitcast(E4M3X4),
+                scales=g_scales[:, s, c0 : c0 + cn],
+                in_=g_words[s][:, c0 : c0 + cn, :].rearrange("p n t -> p (n t)"),
             )
 
         dh = {}
 
         def first_product(e, h):
-            cols = slice(e * C + h * HALF, e * C + (h + 1) * HALF)
-            dht = psum.tile([P, H], F32, name="dht")
+            slots = slice(e * C + h * HALF, e * C + (h + 1) * HALF)
+            by_slot = psum2.tile([P, H], F32, name="sum_n")
             for s in range(NPASS):
                 nc.tensor.matmul_mx(
-                    out=dht[:],
-                    lhsT=codes[:, s, cols].bitcast(E4M3X4),
-                    lhsT_scale=scales_g[:, s, cols],
+                    out=by_slot[:],
+                    lhsT=g_codes[:, s, slots].bitcast(E4M3X4),
+                    lhsT_scale=g_scales[:, s, slots],
                     rhs=w2_t[:, e * NPASS + s, :].bitcast(E2M1X4),
                     rhs_scale=w2s_t[:, e * NPASS + s, :],
                     start=(s == 0),
                     stop=(s == NPASS - 1),
                 )
-            turned = ring2.tile([P, 4, P], F32, name="turned")
-            nc.scalar.copy(out=turned[:], in_=dht[:].rearrange("p (q t) -> p t q", t=4))
-            bank = psum4.tile([P, 4, HALF], F32, name="bank")
-            for t in range(4):
-                nc.tensor.transpose(bank[:, t, :], turned[:, t, :], ident[:])
-            dh[e, h] = bank
+            parted = ring2.tile([P, R, P], F32, name="parted")
+            nc.scalar.copy(out=parted[:], in_=by_slot[:].rearrange("p (q t) -> p t q", t=R))
+            turned = psum4.tile([P, R, HALF], F32, name="turned")
+            for t in range(R):
+                nc.tensor.transpose(turned[:, t, :], parted[:, t, :], ident[:])
+            dh[e, h] = turned
 
-        sig_t = keep.tile([P, E, 4, C], F32, name="sig_t")
+        sig_t = keep.tile([P, E, R, C], F32, name="sig_t")
+        nsilu_t = [keep.tile([P, R, C], F32, name=f"nsilu_t{e}", align_bytes=64) for e in range(E)]
+        weighed = [keep.tile([P, R, C], F32, name="weighed0", align_bytes=64)] + nsilu_t[: E - 1]
+        silu_t = g_pass0[:].rearrange("p t n -> p (t n)").rearrange("p (e t n) -> p e t n", e=E, t=R)
 
         def sigmoid(t):
             nc.scalar.activation(sig_t[:, :, t, :], a1_t[:, t, :].rearrange("p (e n) -> p e n", e=E), ACT.Sigmoid)
-
-        nsilu_t = [keep.tile([P, 4, C], F32, name=f"nsilu_t{e}", align_bytes=64) for e in range(E)]
-        weighed = [keep.tile([P, 4, C], F32, name="weighed0", align_bytes=64)] + nsilu_t[: E - 1]
-
-        silu_t = g_first[:].rearrange("p t n -> p (t n)").rearrange("p (e t n) -> p e t n", e=E, t=4)
 
         def nsilu(e):
             nc.scalar.activation(nsilu_t[e][:], a1_t[:, :, e * C : (e + 1) * C], ACT.Silu, scale=-1.0)
@@ -194,99 +192,94 @@ def tile_moe_bdx_glu_silu_kernel(
         factors = {}
 
         def factor(e):
-            f = ring2.tile([P, 4, C], F32, name="f")
+            f = ring2.tile([P, R, C], F32, name="f")
             nc.vector.scalar_tensor_tensor(f[:], nsilu_t[e][:], 1.0, weighed[e][:], SUB, MULT)
             factors[e] = f
 
-        qd = {}
+        def da_of(e, h):
+            return weighed[e][:].rearrange("p t n -> p (t n)").bitcast(BF16).rearrange("p (h j n t) -> p h j n t", h=2, j=2, t=R)[:, h]
 
         def products(e, h):
-            da = weighed[e][:].rearrange("p t n -> p (t n)").bitcast(BF16).rearrange("p (h j n t) -> p h j n t", h=2, j=2, t=4)[:, h]
-            bank = dh[e, h][:].rearrange("p t (c i) -> p c t i", i=4)
-            nc.vector.tensor_tensor(
-                da[:, 1].rearrange("p (c i) t -> p c t i", i=4), silu_t[:, e, :, h * HALF : (h + 1) * HALF].rearrange("p t (c i) -> p c t i", i=4), bank, MULT
-            )
-            f = factors[e][:, :, h * HALF : (h + 1) * HALF]
+            da = da_of(e, h)
+            slots = slice(h * HALF, (h + 1) * HALF)
+            nc.vector.tensor_tensor(by_runs(da[:, 1]), rows_by_runs(silu_t[:, e, :, slots]), rows_by_runs(dh[e, h][:]), MULT)
+            f = factors[e][:, :, slots]
             if e == 0:
-                nc.vector.tensor_tensor(da[:, 0].rearrange("p (c i) t -> p c t i", i=4), f.rearrange("p t (c i) -> p c t i", i=4), bank, MULT)
+                nc.vector.tensor_tensor(by_runs(da[:, 0]), rows_by_runs(f), rows_by_runs(dh[e, h][:]), MULT)
             else:
-                nc.vector.scalar_tensor_tensor(da[:, 0], f.rearrange("p t n -> p n t"), -1.0, dh[e, h][:].rearrange("p t n -> p n t"), MULT, MULT)
-            qd[e, h] = da
-
-        coded = {}
-
-        def quantize_da(e, h):
-            dc = keep.tile([P, 2, HALF], U32, name=f"dc{e}{h}", align_bytes=64)
-            ds = keep.tile([P, 2, HALF], U8, name=f"ds{e}{h}", align_bytes=64)
-            nc.vector.quantize_mx(
-                out=dc[:].rearrange("p j n -> p (j n)").bitcast(E4M3X4),
-                scales=ds[:].rearrange("p j n -> p (j n)"),
-                in_=qd[e, h].rearrange("p j n t -> p (j n t)"),
-            )
-            coded[e, h] = dc, ds
-
-        def second_group(dst, e, h, kt):
-            dc, ds = coded[e, h]
-            for j in range(2):
-                nc.tensor.matmul_mx(
-                    out=dst,
-                    lhsT=w13_t[j][:, e, 2 * P * kt : 2 * P * (kt + 1)].bitcast(E2M1X4),
-                    lhsT_scale=w13s_t[j][:, e, P * kt : P * (kt + 1)],
-                    rhs=dc[:, j, :].bitcast(E4M3X4),
-                    rhs_scale=ds[:, j, :],
-                    start=(j == 0),
-                    stop=(j == 1),
+                nc.vector.scalar_tensor_tensor(
+                    da[:, 0], f.rearrange("p t n -> p n t"), -1.0, dh[e, h][:].rearrange("p t n -> p n t"), MULT, MULT
                 )
 
-        def second(pool, tag, kt, first, count, copy=nc.scalar.copy):
-            acc = pool.tile([P, count, HALF], F32, name=tag)
-            for i in reversed(range(count)):
-                second_group(acc[:, i, :], (first + i) // 2, (first + i) % 2, kt)
-            copy(out=dx_t[kt][:, first * HALF : (first + count) * HALF], in_=acc[:].rearrange("p i n -> p (i n)"))
+        da_coded = {}
 
-        firsts = {}
+        def quantize_da(e, h):
+            da_codes = keep.tile([P, 2, HALF], U32, name=f"da_codes{e}{h}", align_bytes=64)
+            da_scales = keep.tile([P, 2, HALF], U8, name=f"da_scales{e}{h}", align_bytes=64)
+            nc.vector.quantize_mx(
+                out=da_codes[:].rearrange("p j n -> p (j n)").bitcast(E4M3X4),
+                scales=da_scales[:].rearrange("p j n -> p (j n)"),
+                in_=da_of(e, h).rearrange("p j n t -> p (j n t)"),
+            )
+            da_coded[2 * e + h] = da_codes, da_scales
 
-        def fetch_first(kt):
-            r1 = ring3.tile([P, T], F32, name="r1")
-            nc.vector.tensor_copy(r1[:], dx_t[kt][:].indirect(pos1_t[:]))
-            firsts[kt] = r1
+        dx_t = [keep.tile([P, S], F32, name=f"dx_t{kt}") for kt in range(KT)]
 
-        def add_second(kt, c0, cn):
-            o = ring3.tile([P, cn], F32, name="o")
-            nc.vector.tensor_tensor(o[:], dx_t[kt][:].indirect(pos2_t[:, c0 // 16 : (c0 + cn) // 16]), firsts[kt][:, c0 : c0 + cn], ADD)
-            nc.sync.dma_start(out=out[kt * P : (kt + 1) * P, c0 : c0 + cn], in_=o[:])
+        def second_product(pool, tag, blocks, halves, copy=nc.scalar.copy):
+            acc = pool.tile([P, len(blocks), len(halves), HALF], F32, name=tag)
+            for b, kt in enumerate(blocks):
+                for i in reversed(range(len(halves))):
+                    da_codes, da_scales = da_coded[halves[i]]
+                    e = halves[i] // 2
+                    for j in range(2):
+                        nc.tensor.matmul_mx(
+                            out=acc[:, b, i, :],
+                            lhsT=w13_t[j][:, e, 2 * P * kt : 2 * P * (kt + 1)].bitcast(E2M1X4),
+                            lhsT_scale=w13s_t[j][:, e, P * kt : P * (kt + 1)],
+                            rhs=da_codes[:, j, :].bitcast(E4M3X4),
+                            rhs_scale=da_scales[:, j, :],
+                            start=(j == 0),
+                            stop=(j == 1),
+                        )
+            for b, kt in enumerate(blocks):
+                by_half = dx_t[kt][:].rearrange("p (h n) -> p h n", n=HALF)
+                copy(out=by_half[:, halves.start : halves.stop : halves.step, :], in_=acc[:, b])
 
-        for t in range(4):
+        def combine(pieces):
+            firsts = []
+            for kt, c0, cn in pieces:
+                first = ring3.tile([P, cn], F32, name="first")
+                nc.vector.tensor_copy(first[:], dx_t[kt][:].indirect(pos1_t[:, c0 // 16 : (c0 + cn) // 16]))
+                firsts.append(first)
+            for first, (kt, c0, cn) in zip(firsts, pieces):
+                total = ring3.tile([P, cn], F32, name="total")
+                nc.vector.tensor_tensor(total[:], dx_t[kt][:].indirect(pos2_t[:, c0 // 16 : (c0 + cn) // 16]), first[:], ADD)
+                nc.sync.dma_start(out=out[kt * P : (kt + 1) * P, c0 : c0 + cn], in_=total[:])
+
+        for t in range(R):
             for c0, cn in CUTS if t else OPENING:
-                look_up(g_first[:, t, c0 : c0 + cn], 0, t, c0, cn)
-
-        def first_half(i):
-            c0, cn = CUTS[i]
-            interleave(0, g_first[:, :, c0 : c0 + cn], c0, cn)
-
-        for t in range(4):
+                look_up(g_pass0[:, t, c0 : c0 + cn], 0, t, c0, cn)
+        for t in range(R):
             sigmoid(t)
-        first_half(0)
-        first_half(1)
-        first_half(2)
-        g4 = gather_second(*CUTS[0])
-        interleave(1, g4[:], *CUTS[0])
+        for c0, cn in CUTS:
+            interleave(0, g_pass0[:, :, c0 : c0 + cn], c0, cn)
+        g_cut = look_up_pass1(*CUTS[0])
+        interleave(1, g_cut[:], *CUTS[0])
         nsilu(0)
-        g4 = gather_second(*CUTS[1])
-        quantize_g(0, 0, 256)
-        quantize_g(1, 0, 256)
-        interleave(1, g4[:], *CUTS[1])
-        g4 = gather_second(*CUTS[2])
+        g_cut = look_up_pass1(*CUTS[1])
+        quantize_g(0, 0, C)
+        quantize_g(1, 0, C)
+        interleave(1, g_cut[:], *CUTS[1])
+        g_cut = look_up_pass1(*CUTS[2])
         first_product(0, 0)
         first_product(0, 1)
         silu(0)
-        interleave(1, g4[:], *CUTS[2])
+        interleave(1, g_cut[:], *CUTS[2])
         weigh(0)
-        quantize_g(0, 256, 256)
-        quantize_g(1, 256, 512)
+        quantize_g(0, C, C)
+        quantize_g(1, C, 2 * C)
         factor(0)
-        quantize_g(0, 512, 512)
-        dx_t = [keep.tile([P, S], F32, name=f"dx_t{kt}") for kt in range(KT)]
+        quantize_g(0, 2 * C, 2 * C)
         for e in range(E):
             if e + 1 < E:
                 nsilu(e + 1)
@@ -296,27 +289,23 @@ def tile_moe_bdx_glu_silu_kernel(
                 silu(e + 1)
             if e == E - 2:
                 for kt in range(EARLY):
-                    second(psum, "acc", kt, 0, 4)
+                    second_product(psum2, "sum_i", [kt], range(0, 4))
             products(e, 0)
             products(e, 1)
             quantize_da(e, 0)
             if e == 0:
-                quantize_g(1, 768, 256)
+                quantize_g(1, *CUTS[2])
             if e + 1 < E:
                 factor(e + 1)
             quantize_da(e, 1)
             if e == E - 2:
-                for kt in range(EARLY):
-                    second(psum, "acc", kt, 4, 2)
-        second(psum, "dht", 0, 6, 1)
-        second(psum, "dht", 0, 7, 1, nc.vector.tensor_copy)
-        second(psum4, "bank", 1, 6, 2)
-        for kt in range(EARLY, KT):
-            second(psum, "acc", kt, 0, 4)
-            second(psum4, "bank", kt, 4, 4)
-        fetch_first(0)
-        for kt in range(KT - 1):
-            fetch_first(kt + 1)
-            add_second(kt, 0, T)
-        add_second(KT - 1, 0, T - P)
-        add_second(KT - 1, T - P, P)
+                second_product(psum2, "sum_i", range(EARLY), range(2 * e, 2 * e + 2))
+        second_product(psum2, "sum_n", range(EARLY), range(HALVES - 2, HALVES - 1))
+        second_product(psum4, "turned", range(EARLY), range(HALVES - 1, HALVES), nc.vector.tensor_copy)
+        for pair in range(EARLY, KT, 2):
+            for kt in (pair + 1, pair):
+                second_product(psum4, "turned", [kt], range(1, HALVES, 2))
+                second_product(psum2, "sum_n", [kt], range(0, HALVES, 2))
+        for pair in range(0, KT - 2, 2):
+            combine([(pair, 0, T), (pair + 1, 0, T)])
+        combine([(KT - 2, 0, T), (KT - 1, 0, T - P), (KT - 1, T - P, P)])

@@ -163,7 +163,7 @@ def tile_moe_bdx_glu_silu_kernel(
                     stop=(s == NPASS - 1),
                 )
             parted = ring2.tile([P, R, P], F32, name="parted")
-            nc.scalar.copy(out=parted[:], in_=by_slot[:].rearrange("p (q t) -> p t q", t=R))
+            nc.scalar.activation(parted[:], by_slot[:].rearrange("p (q t) -> p t q", t=R), ACT.Copy, scale=-1.0 if e else 1.0)
             turned = psum4.tile([P, R, HALF], F32, name="turned")
             for t in range(R):
                 nc.tensor.transpose(turned[:, t, :], parted[:, t, :], ident[:])
@@ -173,6 +173,7 @@ def tile_moe_bdx_glu_silu_kernel(
         nsilu_t = [keep.tile([P, R, C], F32, name=f"nsilu_t{e}", align_bytes=64) for e in range(E)]
         weighed = [keep.tile([P, R, C], F32, name="weighed0", align_bytes=64)] + nsilu_t[: E - 1]
         silu_t = g_pass0[:].rearrange("p t n -> p (t n)").rearrange("p (e t n) -> p e t n", e=E, t=R)
+        silu_by_slot = g_pass0[:].rearrange("p t n -> p (t n)").rearrange("p (e n t) -> p e n t", e=E, t=R)
 
         def sigmoid(t):
             nc.scalar.activation(sig_t[:, :, t, :], a1_t[:, t, :].rearrange("p (e n) -> p e n", e=E), ACT.Sigmoid)
@@ -181,7 +182,11 @@ def tile_moe_bdx_glu_silu_kernel(
             nc.scalar.activation(nsilu_t[e][:], a1_t[:, :, e * C : (e + 1) * C], ACT.Silu, scale=-1.0)
 
         def silu(e):
-            nc.scalar.activation(silu_t[:, e], a1_t[:, :, e * C : (e + 1) * C], ACT.Silu)
+            src = a1_t[:, :, e * C : (e + 1) * C]
+            if e == 0:
+                nc.scalar.activation(silu_t[:, e], src, ACT.Silu)
+            else:
+                nc.scalar.activation(by_runs(silu_by_slot[:, e]), rows_by_runs(src), ACT.Silu)
 
         def weigh(e):
             if e == 0:
@@ -202,14 +207,14 @@ def tile_moe_bdx_glu_silu_kernel(
         def products(e, h):
             da = da_of(e, h)
             slots = slice(h * HALF, (h + 1) * HALF)
-            nc.vector.tensor_tensor(by_runs(da[:, 1]), rows_by_runs(silu_t[:, e, :, slots]), rows_by_runs(dh[e, h][:]), MULT)
-            f = factors[e][:, :, slots]
             if e == 0:
-                nc.vector.tensor_tensor(by_runs(da[:, 0]), rows_by_runs(f), rows_by_runs(dh[e, h][:]), MULT)
+                nc.vector.tensor_tensor(by_runs(da[:, 1]), rows_by_runs(silu_t[:, e, :, slots]), rows_by_runs(dh[e, h][:]), MULT)
             else:
                 nc.vector.scalar_tensor_tensor(
-                    da[:, 0], f.rearrange("p t n -> p n t"), -1.0, dh[e, h][:].rearrange("p t n -> p n t"), MULT, MULT
+                    da[:, 1], silu_by_slot[:, e, slots, :], -1.0, dh[e, h][:].rearrange("p t n -> p n t"), MULT, MULT
                 )
+            f = factors[e][:, :, slots]
+            nc.vector.tensor_tensor(by_runs(da[:, 0]), rows_by_runs(f), rows_by_runs(dh[e, h][:]), MULT)
 
         da_coded = {}
 

@@ -31,6 +31,7 @@ KT = K // P
 RUN = 4
 CUTS = ((0, 384), (384, 384), (768, 256))
 OPENING = ((0, 128), (128, 448), (576, 448))
+WIDE = S + 16
 EARLY = 2
 
 
@@ -48,7 +49,7 @@ def tile_moe_bdx_glu_silu_kernel(
         offs_t = keep.tile([P, S // 16], U16, name="offs_t")
         pos1_t = keep.tile([P, T // 16], U16, name="pos1_t")
         pos2_t = keep.tile([P, T // 16], U16, name="pos2_t")
-        dy = [[keep.tile([P, T], F32, name=f"dy{s}{t}") for t in range(R)] for s in range(NPASS)]
+        dy = [[keep.tile([P, WIDE if s == 0 and t else T], F32, name=f"dy{s}{t}") for t in range(R)] for s in range(NPASS)]
         gate_t = keep.tile([P, S], F32, name="gate_t")
         a1_t = keep.tile([P, R, S], F32, name="a1_t")
         a3_t = [keep.tile([P, R, C], F32, name=f"a3_t{e}") for e in range(E)]
@@ -58,14 +59,16 @@ def tile_moe_bdx_glu_silu_kernel(
         w13s_t = [keep.tile([P, E, K], U8, name=f"w13s_t{j}", align_bytes=64) for j in range(2)]
         ident = keep.tile([P, P], F32, name="ident")
 
+        make_identity(nc, ident[:])
         nc.gpsimd.memset(w2s_t[:].bitcast(I32), 0)
         nc.gpsimd.memset(w13s_t[0][:].bitcast(I32), 0)
         nc.gpsimd.memset(w13s_t[1][:].bitcast(I32), 0)
-        make_identity(nc, ident[:])
+        for spare in dy[0][1:]:
+            nc.vector.memset(spare[:, T:], 0.0)
 
         def load_dy(s, t):
             rows = dyT[P * R * s : P * R * (s + 1), :].rearrange("(p t) n -> t p n", t=R)
-            nc.sync.dma_start(out=dy[s][t][:], in_=rows[t])
+            nc.sync.dma_start(out=dy[s][t][:, :T], in_=rows[t])
 
         def load_gate(queue, c0, cn):
             queue.dma_start(out=gate_t[:, c0 : c0 + cn], in_=gate[0:P, c0 : c0 + cn])
@@ -262,15 +265,15 @@ def tile_moe_bdx_glu_silu_kernel(
                 nc.sync.dma_start(out=out[kt * P : (kt + 1) * P, c0 : c0 + cn], in_=total[:])
 
         for t in range(R):
-            for c0, cn in CUTS if t else OPENING:
+            for c0, cn in ((0, S),) if t else OPENING:
                 look_up(g_pass0[:, t, c0 : c0 + cn], 0, t, c0, cn)
         for t in range(R):
             sigmoid(t)
+        nsilu(0)
         for c0, cn in CUTS:
             interleave(0, g_pass0[:, :, c0 : c0 + cn], c0, cn)
         g_cut = look_up_pass1(*CUTS[0])
         interleave(1, g_cut[:], *CUTS[0])
-        nsilu(0)
         g_cut = look_up_pass1(*CUTS[1])
         quantize_g(0, 0, C)
         quantize_g(1, 0, C)

@@ -29,7 +29,7 @@ HALVES = S // HALF
 NPASS = N // (P * R)
 KT = K // P
 RUN = 4
-CUTS = ((0, 384), (384, 384), (768, 256))
+CUTS = ((0, 256), (256, 384), (640, 384))
 OPENING = ((0, 128), (128, 448), (576, 448))
 WIDE = S + 16
 EARLY = 2
@@ -166,72 +166,71 @@ def tile_moe_bdx_glu_silu_kernel(
                     stop=(s == NPASS - 1),
                 )
             parted = ring2.tile([P, R, P], F32, name="parted")
-            nc.scalar.activation(parted[:], by_slot[:].rearrange("p (q t) -> p t q", t=R), ACT.Copy, scale=-1.0 if e else 1.0)
+            nc.scalar.activation(parted[:], by_slot[:].rearrange("p (q t) -> p t q", t=R), ACT.Copy, scale=-1.0)
             turned = psum4.tile([P, R, HALF], F32, name="turned")
             for t in range(R):
                 nc.tensor.transpose(turned[:, t, :], parted[:, t, :], ident[:])
             dh[e, h] = turned
 
         sig_t = keep.tile([P, E, R, C], F32, name="sig_t")
-        nsilu_t = [keep.tile([P, R, C], F32, name=f"nsilu_t{e}", align_bytes=64) for e in range(E)]
-        weighed = [keep.tile([P, R, C], F32, name="weighed0", align_bytes=64)] + nsilu_t[: E - 1]
-        silu_t = g_pass0[:].rearrange("p t n -> p (t n)").rearrange("p (e t n) -> p e t n", e=E, t=R)
+        nsilu_t = {}
         silu_by_slot = g_pass0[:].rearrange("p t n -> p (t n)").rearrange("p (e n t) -> p e n t", e=E, t=R)
 
         def sigmoid(t):
             nc.scalar.activation(sig_t[:, :, t, :], a1_t[:, t, :].rearrange("p (e n) -> p e n", e=E), ACT.Sigmoid)
 
         def nsilu(e):
+            nsilu_t[e] = ring2.tile([P, R, C], F32, name="nsilu_t")
             nc.scalar.activation(nsilu_t[e][:], a1_t[:, :, e * C : (e + 1) * C], ACT.Silu, scale=-1.0)
 
         def silu(e):
-            src = a1_t[:, :, e * C : (e + 1) * C]
-            if e == 0:
-                nc.scalar.activation(silu_t[:, e], src, ACT.Silu)
-            else:
-                nc.scalar.activation(by_runs(silu_by_slot[:, e]), rows_by_runs(src), ACT.Silu)
+            nc.scalar.activation(by_runs(silu_by_slot[:, e]), rows_by_runs(a1_t[:, :, e * C : (e + 1) * C]), ACT.Silu)
+
+        weighed = {}
+        work = {}
 
         def weigh(e):
             if e == 0:
-                nc.vector.scalar_tensor_tensor(weighed[e][:], sig_t[:, e], -1.0, a3_t[e][:], MULT, MULT)
+                weighed[e] = keep.tile([P, R, C], F32, name="weighed0", tag=f"dy1{R - 1}")[:]
             else:
-                nc.gpsimd.tensor_tensor(weighed[e][:], sig_t[:, e], a3_t[e][:], MULT)
+                weighed[e] = work[e - 1, 0][:].rearrange("p (t n) -> p t n", t=R)
+            nc.gpsimd.tensor_tensor(weighed[e], sig_t[:, e], a3_t[e][:], MULT)
 
-        factors = {}
-
-        def factor(e):
-            f = ring2.tile([P, R, C], F32, name="f")
-            nc.vector.scalar_tensor_tensor(f[:], nsilu_t[e][:], 1.0, weighed[e][:], SUB, MULT)
-            factors[e] = f
+        def partial_of(e, h):
+            return work[e, h][:, : R * HALF].rearrange("p (t n) -> p t n", t=R)
 
         def da_of(e, h):
-            return weighed[e][:].rearrange("p t n -> p (t n)").bitcast(BF16).rearrange("p (h j n t) -> p h j n t", h=2, j=2, t=R)[:, h]
+            return work[e, h][:, R * HALF :].bitcast(BF16).rearrange("p (j n t) -> p j n t", j=2, t=R)
 
-        def products(e, h):
-            da = da_of(e, h)
-            slots = slice(h * HALF, (h + 1) * HALF)
-            if e == 0:
-                nc.vector.tensor_tensor(by_runs(da[:, 1]), rows_by_runs(silu_t[:, e, :, slots]), rows_by_runs(dh[e, h][:]), MULT)
+        def from_psum(e, h):
+            if h == 0:
+                work[e, h] = keep.tile([P, R * C], F32, name=f"work{e}", align_bytes=64)
             else:
-                nc.vector.scalar_tensor_tensor(
-                    da[:, 1], silu_by_slot[:, e, slots, :], -1.0, dh[e, h][:].rearrange("p t n -> p n t"), MULT, MULT
-                )
-            f = factors[e][:, :, slots]
-            nc.vector.tensor_tensor(by_runs(da[:, 0]), rows_by_runs(f), rows_by_runs(dh[e, h][:]), MULT)
+                work[e, h] = ring2.tile([P, R * C], F32, name="work", align_bytes=64)
+            slots = slice(h * HALF, (h + 1) * HALF)
+            nc.vector.scalar_tensor_tensor(partial_of(e, h), nsilu_t[e][:, :, slots], 1.0, dh[e, h][:], SUB, MULT)
+            nc.vector.scalar_tensor_tensor(
+                da_of(e, h)[:, 1], silu_by_slot[:, e, slots, :], -1.0, dh[e, h][:].rearrange("p t n -> p n t"), MULT, MULT
+            )
+
+        def product_da1(e, h):
+            factor = weighed[e][:, :, h * HALF : (h + 1) * HALF]
+            nc.vector.tensor_tensor(by_runs(da_of(e, h)[:, 0]), rows_by_runs(partial_of(e, h)), rows_by_runs(factor), MULT)
 
         da_coded = {}
 
         def quantize_da(e, h):
             da_codes = keep.tile([P, 2, HALF], U32, name=f"da_codes{e}{h}", align_bytes=64)
             da_scales = keep.tile([P, 2, HALF], U8, name=f"da_scales{e}{h}", align_bytes=64)
-            nc.vector.quantize_mx(
-                out=da_codes[:].rearrange("p j n -> p (j n)").bitcast(E4M3X4),
-                scales=da_scales[:].rearrange("p j n -> p (j n)"),
-                in_=da_of(e, h).rearrange("p j n t -> p (j n t)"),
-            )
+            for js in (slice(1, 2), slice(0, 1)) if 2 * e + h == HALVES - 1 else (slice(0, 2),):
+                nc.vector.quantize_mx(
+                    out=da_codes[:, js].rearrange("p j n -> p (j n)").bitcast(E4M3X4),
+                    scales=da_scales[:, js].rearrange("p j n -> p (j n)"),
+                    in_=da_of(e, h)[:, js].rearrange("p j n t -> p (j n t)"),
+                )
             da_coded[2 * e + h] = da_codes, da_scales
 
-        dx_t = [keep.tile([P, S], F32, name=f"dx_t{kt}") for kt in range(KT)]
+        dx_t = [keep.tile([P, S], F32, name=f"dx_t{kt}", tag=f"dy0{kt - 2}" if kt > 2 else f"dx_t{kt}") for kt in range(KT)]
 
         def second_product(pool, tag, blocks, halves, copy=nc.scalar.copy):
             acc = pool.tile([P, len(blocks), len(halves), HALF], F32, name=tag)
@@ -239,15 +238,15 @@ def tile_moe_bdx_glu_silu_kernel(
                 for i in reversed(range(len(halves))):
                     da_codes, da_scales = da_coded[halves[i]]
                     e = halves[i] // 2
-                    for j in range(2):
+                    for j in (1, 0):
                         nc.tensor.matmul_mx(
                             out=acc[:, b, i, :],
                             lhsT=w13_t[j][:, e, 2 * P * kt : 2 * P * (kt + 1)].bitcast(E2M1X4),
                             lhsT_scale=w13s_t[j][:, e, P * kt : P * (kt + 1)],
                             rhs=da_codes[:, j, :].bitcast(E4M3X4),
                             rhs_scale=da_scales[:, j, :],
-                            start=(j == 0),
-                            stop=(j == 1),
+                            start=(j == 1),
+                            stop=(j == 0),
                         )
             for b, kt in enumerate(blocks):
                 by_half = dx_t[kt][:].rearrange("p (h n) -> p h n", n=HALF)
@@ -260,7 +259,7 @@ def tile_moe_bdx_glu_silu_kernel(
                 nc.vector.tensor_copy(first[:], dx_t[kt][:].indirect(pos1_t[:, c0 // 16 : (c0 + cn) // 16]))
                 firsts.append(first)
             for first, (kt, c0, cn) in zip(firsts, pieces):
-                total = ring3.tile([P, cn], F32, name="total")
+                total = keep.tile([P, cn], F32, name=f"total{kt}_{c0}")
                 nc.vector.tensor_tensor(total[:], dx_t[kt][:].indirect(pos2_t[:, c0 // 16 : (c0 + cn) // 16]), first[:], ADD)
                 nc.sync.dma_start(out=out[kt * P : (kt + 1) * P, c0 : c0 + cn], in_=total[:])
 
@@ -278,38 +277,37 @@ def tile_moe_bdx_glu_silu_kernel(
         quantize_g(0, 0, C)
         quantize_g(1, 0, C)
         interleave(1, g_cut[:], *CUTS[1])
+        quantize_g(0, C, C)
+        quantize_g(0, 2 * C, 2 * C)
+        quantize_g(1, C, C)
         g_cut = look_up_pass1(*CUTS[2])
         first_product(0, 0)
         first_product(0, 1)
         silu(0)
         interleave(1, g_cut[:], *CUTS[2])
-        weigh(0)
-        quantize_g(0, C, C)
-        quantize_g(1, C, 2 * C)
-        factor(0)
-        quantize_g(0, 2 * C, 2 * C)
         for e in range(E):
+            weigh(e)
             if e + 1 < E:
                 nsilu(e + 1)
-                weigh(e + 1)
                 first_product(e + 1, 0)
                 first_product(e + 1, 1)
                 silu(e + 1)
             if e == E - 2:
                 for kt in range(EARLY):
                     second_product(psum2, "sum_i", [kt], range(0, 4))
-            products(e, 0)
-            products(e, 1)
-            quantize_da(e, 0)
+            from_psum(e, 0)
+            from_psum(e, 1)
+            product_da1(e, 0)
+            product_da1(e, 1)
             if e == 0:
-                quantize_g(1, *CUTS[2])
-            if e + 1 < E:
-                factor(e + 1)
+                quantize_g(1, 2 * C, 2 * C)
+            quantize_da(e, 0)
             quantize_da(e, 1)
             if e == E - 2:
                 second_product(psum2, "sum_i", range(EARLY), range(2 * e, 2 * e + 2))
         second_product(psum2, "sum_n", range(EARLY), range(HALVES - 2, HALVES - 1))
-        second_product(psum4, "turned", range(EARLY), range(HALVES - 1, HALVES), nc.vector.tensor_copy)
+        for kt in range(EARLY):
+            second_product(psum4, "turned", [kt], range(HALVES - 1, HALVES), nc.vector.tensor_copy)
         for pair in range(EARLY, KT, 2):
             for kt in (pair + 1, pair):
                 second_product(psum4, "turned", [kt], range(1, HALVES, 2))

@@ -52,7 +52,7 @@ def tile_moe_bdx_glu_silu_kernel(
         dy = [[keep.tile([P, WIDE if s == 0 and t else T], F32, name=f"dy{s}{t}") for t in range(R)] for s in range(NPASS)]
         gate_t = keep.tile([P, S], F32, name="gate_t")
         a1_t = keep.tile([P, R, S], F32, name="a1_t")
-        a3_t = [keep.tile([P, R, C], F32, name=f"a3_t{e}") for e in range(E)]
+        a3_t = [keep.tile([P, R, C], F32, name=f"a3_t{e}", align_bytes=64) for e in range(E)]
         w2_t = keep.tile([P, E * NPASS, 2 * H], U8, name="w2_t", align_bytes=64)
         w2s_t = keep.tile([P, E * NPASS, H], U8, name="w2s_t", align_bytes=64)
         w13_t = [keep.tile([P, E, 2 * K], U8, name=f"w13_t{j}", align_bytes=64) for j in range(2)]
@@ -118,8 +118,6 @@ def tile_moe_bdx_glu_silu_kernel(
         nc.sync.dma_start(pos1_t[:], pos1)
         nc.sync.dma_start(pos2_t[:], pos2)
 
-        g_codes = keep.tile([P, NPASS, S], U32, name="g_codes", align_bytes=64)
-        g_scales = keep.tile([P, NPASS, S], U8, name="g_scales", align_bytes=64)
         g_words = [keep.tile([P, S, R], BF16, name=f"g_words{s}", align_bytes=64) for s in range(NPASS)]
         g_pass0 = keep.tile([P, R, S], F32, name="g_pass0")
 
@@ -143,23 +141,32 @@ def tile_moe_bdx_glu_silu_kernel(
         def interleave(s, src, c0, cn):
             nc.scalar.copy(out=by_runs(g_words[s][:, c0 : c0 + cn, :]), in_=rows_by_runs(src))
 
-        def quantize_g(s, c0, cn):
+        g_coded = {}
+
+        def quantize_g(s, experts, tag=""):
+            c0, cn = experts.start * C, len(experts) * C
+            codes = keep.tile([P, cn], U32, name=f"g_codes{s}{experts.start}", tag=tag, align_bytes=64)
+            scales = keep.tile([P, cn], U8, name=f"g_scales{s}{experts.start}", align_bytes=64)
             nc.vector.quantize_mx(
-                out=g_codes[:, s, c0 : c0 + cn].bitcast(E4M3X4),
-                scales=g_scales[:, s, c0 : c0 + cn],
+                out=codes[:].bitcast(E4M3X4),
+                scales=scales[:],
                 in_=g_words[s][:, c0 : c0 + cn, :].rearrange("p n t -> p (n t)"),
             )
+            for e in experts:
+                own = slice(e * C - c0, (e + 1) * C - c0)
+                g_coded[s, e] = codes[:, own], scales[:, own]
 
         dh = {}
 
         def first_product(e, h):
-            slots = slice(e * C + h * HALF, e * C + (h + 1) * HALF)
+            slots = slice(h * HALF, (h + 1) * HALF)
             by_slot = psum2.tile([P, H], F32, name="sum_n")
             for s in range(NPASS):
+                codes, scales = g_coded[s, e]
                 nc.tensor.matmul_mx(
                     out=by_slot[:],
-                    lhsT=g_codes[:, s, slots].bitcast(E4M3X4),
-                    lhsT_scale=g_scales[:, s, slots],
+                    lhsT=codes[:, slots].bitcast(E4M3X4),
+                    lhsT_scale=scales[:, slots],
                     rhs=w2_t[:, e * NPASS + s, :].bitcast(E2M1X4),
                     rhs_scale=w2s_t[:, e * NPASS + s, :],
                     start=(s == 0),
@@ -174,26 +181,25 @@ def tile_moe_bdx_glu_silu_kernel(
 
         sig_t = keep.tile([P, E, R, C], F32, name="sig_t")
         nsilu_t = {}
-        silu_by_slot = g_pass0[:].rearrange("p t n -> p (t n)").rearrange("p (e n t) -> p e n t", e=E, t=R)
+        nsilu_tags = ("nsilu_even", "nsilu_odd", "nsilu_even", "a3_t1")
+        silu_t = {}
 
         def sigmoid(t):
             nc.scalar.activation(sig_t[:, :, t, :], a1_t[:, t, :].rearrange("p (e n) -> p e n", e=E), ACT.Sigmoid)
 
         def nsilu(e):
-            nsilu_t[e] = ring2.tile([P, R, C], F32, name="nsilu_t")
+            nsilu_t[e] = keep.tile([P, R, C], F32, name=f"nsilu_t{e}", tag=nsilu_tags[e], align_bytes=64)
             nc.scalar.activation(nsilu_t[e][:], a1_t[:, :, e * C : (e + 1) * C], ACT.Silu, scale=-1.0)
 
         def silu(e):
-            nc.scalar.activation(by_runs(silu_by_slot[:, e]), rows_by_runs(a1_t[:, :, e * C : (e + 1) * C]), ACT.Silu)
+            silu_t[e] = ring2.tile([P, C, R], F32, name="silu_t")
+            nc.scalar.activation(by_runs(silu_t[e][:]), rows_by_runs(a1_t[:, :, e * C : (e + 1) * C]), ACT.Silu)
 
         weighed = {}
         work = {}
 
         def weigh(e):
-            if e == 0:
-                weighed[e] = keep.tile([P, R, C], F32, name="weighed0", tag=f"dy1{R - 1}")[:]
-            else:
-                weighed[e] = work[e - 1, 0][:].rearrange("p (t n) -> p t n", t=R)
+            weighed[e] = keep.tile([P, R, C], F32, name=f"weighed{e}", tag=f"dy1{R - 1}")[:]
             nc.gpsimd.tensor_tensor(weighed[e], sig_t[:, e], a3_t[e][:], MULT)
 
         def partial_of(e, h):
@@ -203,14 +209,11 @@ def tile_moe_bdx_glu_silu_kernel(
             return work[e, h][:, R * HALF :].bitcast(BF16).rearrange("p (j n t) -> p j n t", j=2, t=R)
 
         def from_psum(e, h):
-            if h == 0:
-                work[e, h] = keep.tile([P, R * C], F32, name=f"work{e}", align_bytes=64)
-            else:
-                work[e, h] = ring2.tile([P, R * C], F32, name="work", align_bytes=64)
+            work[e, h] = ring3.tile([P, R * C], F32, name="work", align_bytes=64)
             slots = slice(h * HALF, (h + 1) * HALF)
             nc.vector.scalar_tensor_tensor(partial_of(e, h), nsilu_t[e][:, :, slots], 1.0, dh[e, h][:], SUB, MULT)
             nc.vector.scalar_tensor_tensor(
-                da_of(e, h)[:, 1], silu_by_slot[:, e, slots, :], -1.0, dh[e, h][:].rearrange("p t n -> p n t"), MULT, MULT
+                da_of(e, h)[:, 1], silu_t[e][:, slots, :], -1.0, dh[e, h][:].rearrange("p t n -> p n t"), MULT, MULT
             )
 
         def product_da1(e, h):
@@ -220,7 +223,8 @@ def tile_moe_bdx_glu_silu_kernel(
         da_coded = {}
 
         def quantize_da(e, h):
-            da_codes = keep.tile([P, 2, HALF], U32, name=f"da_codes{e}{h}", align_bytes=64)
+            tag = nsilu_tags[e + 1] if h == 1 and e + 1 < E else f"da_codes{e}{h}"
+            da_codes = keep.tile([P, 2, HALF], U32, name=f"da_codes{e}{h}", tag=tag, align_bytes=64)
             da_scales = keep.tile([P, 2, HALF], U8, name=f"da_scales{e}{h}", align_bytes=64)
             for js in (slice(1, 2), slice(0, 1)) if 2 * e + h == HALVES - 1 else (slice(0, 2),):
                 nc.vector.quantize_mx(
@@ -259,7 +263,7 @@ def tile_moe_bdx_glu_silu_kernel(
                 nc.vector.tensor_copy(first[:], dx_t[kt][:].indirect(pos1_t[:, c0 // 16 : (c0 + cn) // 16]))
                 firsts.append(first)
             for first, (kt, c0, cn) in zip(firsts, pieces):
-                total = keep.tile([P, cn], F32, name=f"total{kt}_{c0}")
+                total = keep.tile([P, cn], F32, name=f"total{kt}_{c0}", tag=f"dy1{kt}" if kt < R - 1 else f"total{kt}_{c0}")
                 nc.vector.tensor_tensor(total[:], dx_t[kt][:].indirect(pos2_t[:, c0 // 16 : (c0 + cn) // 16]), first[:], ADD)
                 nc.sync.dma_start(out=out[kt * P : (kt + 1) * P, c0 : c0 + cn], in_=total[:])
 
@@ -274,13 +278,13 @@ def tile_moe_bdx_glu_silu_kernel(
         g_cut = look_up_pass1(*CUTS[0])
         interleave(1, g_cut[:], *CUTS[0])
         g_cut = look_up_pass1(*CUTS[1])
-        quantize_g(0, 0, C)
-        quantize_g(1, 0, C)
+        quantize_g(0, range(0, 1))
+        quantize_g(1, range(0, 1))
         interleave(1, g_cut[:], *CUTS[1])
-        quantize_g(0, C, C)
-        quantize_g(0, 2 * C, 2 * C)
-        quantize_g(1, C, C)
+        quantize_g(0, range(1, 2))
+        quantize_g(0, range(2, 4))
         g_cut = look_up_pass1(*CUTS[2])
+        quantize_g(1, range(1, 2))
         first_product(0, 0)
         first_product(0, 1)
         silu(0)
@@ -292,19 +296,21 @@ def tile_moe_bdx_glu_silu_kernel(
                 first_product(e + 1, 0)
                 first_product(e + 1, 1)
                 silu(e + 1)
+            from_psum(e, 0)
+            from_psum(e, 1)
+            if e:
+                quantize_da(e - 1, 1)
             if e == E - 2:
                 for kt in range(EARLY):
                     second_product(psum2, "sum_i", [kt], range(0, 4))
-            from_psum(e, 0)
-            from_psum(e, 1)
+            if e == E - 1:
+                second_product(psum2, "sum_i", range(EARLY), range(2 * e - 2, 2 * e))
             product_da1(e, 0)
-            product_da1(e, 1)
             if e == 0:
-                quantize_g(1, 2 * C, 2 * C)
+                quantize_g(1, range(2, 4), "a3_t0")
+            product_da1(e, 1)
             quantize_da(e, 0)
-            quantize_da(e, 1)
-            if e == E - 2:
-                second_product(psum2, "sum_i", range(EARLY), range(2 * e, 2 * e + 2))
+        quantize_da(E - 1, 1)
         second_product(psum2, "sum_n", range(EARLY), range(HALVES - 2, HALVES - 1))
         for kt in range(EARLY):
             second_product(psum4, "turned", [kt], range(HALVES - 1, HALVES), nc.vector.tensor_copy)

@@ -29,10 +29,9 @@ HALVES = S // HALF
 NPASS = N // (P * R)
 KT = K // P
 RUN = 4
-CUTS = ((0, 256), (256, 384), (640, 384))
-OPENING = ((0, 128), (128, 448), (576, 448))
-WIDE = S + 16
-EARLY = 2
+PAIR = 2 * C
+WIDE = PAIR + 16
+OPENING = ((0, 128), (128, PAIR - 128))
 
 
 def tile_moe_bdx_glu_silu_kernel(
@@ -46,35 +45,40 @@ def tile_moe_bdx_glu_silu_kernel(
         psum2 = ctx.enter_context(tc.psum_pool(name="psum2", bufs=2))
         psum4 = ctx.enter_context(tc.psum_pool(name="psum4", bufs=4))
 
+        def held(shape, dtype, name, tag=""):
+            return keep.tile(shape, dtype, name=name, tag=tag or name, align_bytes=64)
+
         offs_t = keep.tile([P, S // 16], U16, name="offs_t")
         pos1_t = keep.tile([P, T // 16], U16, name="pos1_t")
         pos2_t = keep.tile([P, T // 16], U16, name="pos2_t")
-        dy = [[keep.tile([P, WIDE if s == 0 and t else T], F32, name=f"dy{s}{t}") for t in range(R)] for s in range(NPASS)]
-        gate_t = keep.tile([P, S], F32, name="gate_t")
-        a1_t = keep.tile([P, R, S], F32, name="a1_t")
-        a3_t = [keep.tile([P, R, C], F32, name=f"a3_t{e}", align_bytes=64) for e in range(E)]
-        w2_t = keep.tile([P, E * NPASS, 2 * H], U8, name="w2_t", align_bytes=64)
-        w2s_t = keep.tile([P, E * NPASS, H], U8, name="w2s_t", align_bytes=64)
-        w13_t = [keep.tile([P, E, 2 * K], U8, name=f"w13_t{j}", align_bytes=64) for j in range(2)]
-        w13s_t = [keep.tile([P, E, K], U8, name=f"w13s_t{j}", align_bytes=64) for j in range(2)]
-        ident = keep.tile([P, P], F32, name="ident")
+        dy = [[held([P, WIDE], F32, f"dy{s}{t}") for t in range(R)] for s in range(NPASS)]
+        gate_pair = held([P, PAIR], F32, "gate_pair")
+        gate_t = {e: held([P, C], F32, f"gate{e}") for e in (2, 3)}
+        a1_t = held([P, R, S], F32, "a1_t")
+        a3_t = [held([P, R, C], F32, f"a3_t{e}") for e in range(E)]
+        w2_t = held([P, E * NPASS, 2 * H], U8, "w2_t")
+        w2s_t = held([P, E * NPASS, H], U8, "w2s_t")
+        w13_t = [held([P, E, 2 * K], U8, f"w13_t{j}") for j in range(2)]
+        w13s_t = [held([P, E, K], U8, f"w13s_t{j}") for j in range(2)]
+        ident = held([P, P], F32, "ident")
 
         make_identity(nc, ident[:])
         nc.gpsimd.memset(w2s_t[:].bitcast(I32), 0)
         nc.gpsimd.memset(w13s_t[0][:].bitcast(I32), 0)
         nc.gpsimd.memset(w13s_t[1][:].bitcast(I32), 0)
-        for spare in dy[0][1:]:
-            nc.vector.memset(spare[:, T:], 0.0)
+        for window in dy[0] + dy[1]:
+            nc.vector.memset(window[:, T:], 0.0)
 
         def load_dy(s, t):
             rows = dyT[P * R * s : P * R * (s + 1), :].rearrange("(p t) n -> t p n", t=R)
             nc.sync.dma_start(out=dy[s][t][:, :T], in_=rows[t])
 
-        def load_gate(queue, c0, cn):
-            queue.dma_start(out=gate_t[:, c0 : c0 + cn], in_=gate[0:P, c0 : c0 + cn])
+        def load_gate(queue, dst, c0, cn):
+            queue.dma_start(out=dst, in_=gate[0:P, c0 : c0 + cn])
 
-        def load_a1(t):
-            nc.sync.dma_start(out=a1_t[:, t, :], in_=a1.rearrange("(p t) n -> t p n", t=R)[t])
+        def load_a1(pair, t):
+            cols = slice(pair * PAIR, (pair + 1) * PAIR)
+            nc.sync.dma_start(out=a1_t[:, t, cols], in_=a1.rearrange("(p t) n -> t p n", t=R)[t][:, cols])
 
         def load_a3(e):
             nc.sync.dma_start(out=a3_t[e][:], in_=a3.rearrange("(p t) n -> p t n", t=R)[:, :, e * C : (e + 1) * C])
@@ -89,26 +93,23 @@ def tile_moe_bdx_glu_silu_kernel(
             for r in range(4):
                 nc.sync.dma_start(out=dst[:].bitcast(I32)[r : P : 32, :, :], in_=view[r])
 
-        load_gate(nc.scalar, *OPENING[0])
+        (c0, cn), (c1, cm) = OPENING
+        load_gate(nc.scalar, gate_pair[:, c0 : c0 + cn], c0, cn)
         load_dy(0, 0)
         nc.sync.dma_start(offs_t[:], offs)
-        for c0, cn in OPENING[1:]:
-            load_gate(nc.sync, c0, cn)
-        load_dy(0, 1)
-        load_a1(0)
-        load_dy(0, 2)
-        load_a1(1)
-        load_a1(2)
-        load_dy(0, 3)
-        load_a1(3)
-        for t in range(R):
-            load_dy(1, t)
+        load_gate(nc.sync, gate_pair[:, c1 : c1 + cm], c1, cm)
+        for m in range(NPASS * R):
+            if m + 1 < NPASS * R:
+                load_dy(*divmod(m + 1, R))
+            load_a1(*divmod(m, R))
         load_w2(0)
         load_scales(w2s_t, w2_scales)
-        load_a3(0)
+        load_gate(nc.sync, gate_t[2][:], 2 * C, C)
         load_w2(1)
-        load_a3(1)
+        load_a3(0)
         load_w2(2)
+        load_gate(nc.sync, gate_t[3][:], 3 * C, C)
+        load_a3(1)
         load_w2(3)
         load_a3(2)
         for j, (words, scales) in enumerate(((w1_words, w1_scales), (w3_words, w3_scales))):
@@ -118,43 +119,46 @@ def tile_moe_bdx_glu_silu_kernel(
         nc.sync.dma_start(pos1_t[:], pos1)
         nc.sync.dma_start(pos2_t[:], pos2)
 
-        g_words = [keep.tile([P, S, R], BF16, name=f"g_words{s}", align_bytes=64) for s in range(NPASS)]
-        g_pass0 = keep.tile([P, R, S], F32, name="g_pass0")
-
-        def look_up(dst, s, t, c0, cn):
-            nc.vector.tensor_tensor(
-                dst, dy[s][t][:].indirect(offs_t[:, c0 // 16 : (c0 + cn) // 16]), gate_t[:, c0 : c0 + cn], MULT
-            )
-
-        def look_up_pass1(c0, cn):
-            g_cut = ring2.tile([P, R, cn], F32, name="g_cut")
-            for t in range(R):
-                look_up(g_cut[:, t, :], 1, t, c0, cn)
-            return g_cut
-
         def by_runs(slot_major):
             return slot_major.rearrange("p (c i) t -> p c t i", i=RUN)
 
         def rows_by_runs(residue_major):
             return residue_major.rearrange("p t (c i) -> p c t i", i=RUN)
 
-        def interleave(s, src, c0, cn):
-            nc.scalar.copy(out=by_runs(g_words[s][:, c0 : c0 + cn, :]), in_=rows_by_runs(src))
-
+        gated = [held([P, R, PAIR], F32, f"gated{s}") for s in range(NPASS)]
+        plain = {}
+        g_words = {}
         g_coded = {}
 
-        def quantize_g(s, experts, tag=""):
-            c0, cn = experts.start * C, len(experts) * C
-            codes = keep.tile([P, cn], U32, name=f"g_codes{s}{experts.start}", tag=tag, align_bytes=64)
-            scales = keep.tile([P, cn], U8, name=f"g_scales{s}{experts.start}", align_bytes=64)
-            nc.vector.quantize_mx(
-                out=codes[:].bitcast(E4M3X4),
-                scales=scales[:],
-                in_=g_words[s][:, c0 : c0 + cn, :].rearrange("p n t -> p (n t)"),
+        def look_up_gated(s, t, c0, cn):
+            nc.vector.tensor_tensor(
+                gated[s][:, t, c0 : c0 + cn],
+                dy[s][t][:].indirect(offs_t[:, c0 // 16 : (c0 + cn) // 16]),
+                gate_pair[:, c0 : c0 + cn],
+                MULT,
             )
-            for e in experts:
-                own = slice(e * C - c0, (e + 1) * C - c0)
-                g_coded[s, e] = codes[:, own], scales[:, own]
+
+        def look_up_plain(e, s, t):
+            if t == 0:
+                plain[e, s] = held([P, R, C], F32, f"plain{e}{s}", f"plain{s}")
+            nc.scalar.activation(plain[e, s][:, t, :], dy[s][t][:].indirect(offs_t[:, e * C // 16 : (e + 1) * C // 16]), ACT.Copy)
+
+        def interleave(e, s):
+            g_words[e, s] = held([P, C, R], BF16, f"g_words{e}{s}")
+            nc.vector.tensor_copy(by_runs(g_words[e, s][:]), rows_by_runs(gated[s][:, :, e * C : (e + 1) * C]))
+
+        def apply_gate(e, s, tag=""):
+            g_words[e, s] = held([P, C, R], BF16, f"g_words{e}{s}", tag)
+            spread = gate_t[e][:].rearrange("p (c i) -> p c i", i=RUN).unsqueeze(2).to_broadcast([P, C // RUN, R, RUN])
+            nc.vector.tensor_tensor(by_runs(g_words[e, s][:]), rows_by_runs(plain[e, s][:]), spread, MULT)
+
+        def quantize_g(e, s):
+            codes = held([P, C], U32, f"g_codes{e}{s}")
+            scales = held([P, C], U8, f"g_scales{e}{s}")
+            nc.vector.quantize_mx(
+                out=codes[:].bitcast(E4M3X4), scales=scales[:], in_=g_words[e, s][:].rearrange("p n t -> p (n t)")
+            )
+            g_coded[e, s] = codes, scales
 
         dh = {}
 
@@ -162,7 +166,7 @@ def tile_moe_bdx_glu_silu_kernel(
             slots = slice(h * HALF, (h + 1) * HALF)
             by_slot = psum2.tile([P, H], F32, name="sum_n")
             for s in range(NPASS):
-                codes, scales = g_coded[s, e]
+                codes, scales = g_coded[e, s]
                 nc.tensor.matmul_mx(
                     out=by_slot[:],
                     lhsT=codes[:, slots].bitcast(E4M3X4),
@@ -179,27 +183,34 @@ def tile_moe_bdx_glu_silu_kernel(
                 nc.tensor.transpose(turned[:, t, :], parted[:, t, :], ident[:])
             dh[e, h] = turned
 
-        sig_t = keep.tile([P, E, R, C], F32, name="sig_t")
+        sig_t = held([P, E, R, C], F32, "sig_t")
         nsilu_t = {}
         nsilu_tags = ("nsilu_even", "nsilu_odd", "nsilu_even", "a3_t1")
         silu_t = {}
 
-        def sigmoid(t):
-            nc.scalar.activation(sig_t[:, :, t, :], a1_t[:, t, :].rearrange("p (e n) -> p e n", e=E), ACT.Sigmoid)
+        def sigmoid(pair, t):
+            src = a1_t[:, t, pair * PAIR : (pair + 1) * PAIR].rearrange("p (e n) -> p e n", e=2)
+            nc.scalar.activation(sig_t[:, 2 * pair : 2 * pair + 2, t, :], src, ACT.Sigmoid)
 
         def nsilu(e):
-            nsilu_t[e] = keep.tile([P, R, C], F32, name=f"nsilu_t{e}", tag=nsilu_tags[e], align_bytes=64)
+            nsilu_t[e] = held([P, R, C], F32, f"nsilu_t{e}", nsilu_tags[e])
             nc.scalar.activation(nsilu_t[e][:], a1_t[:, :, e * C : (e + 1) * C], ACT.Silu, scale=-1.0)
 
         def silu(e):
             silu_t[e] = ring2.tile([P, C, R], F32, name="silu_t")
             nc.scalar.activation(by_runs(silu_t[e][:]), rows_by_runs(a1_t[:, :, e * C : (e + 1) * C]), ACT.Silu)
 
+        def prepare(e):
+            nsilu(e)
+            silu(e)
+            first_product(e, 0)
+            first_product(e, 1)
+
         weighed = {}
         work = {}
 
         def weigh(e):
-            weighed[e] = keep.tile([P, R, C], F32, name=f"weighed{e}", tag=f"dy1{R - 1}")[:]
+            weighed[e] = held([P, R, C], F32, f"weighed{e}", f"gate{2 + e // 2}")[:]
             nc.gpsimd.tensor_tensor(weighed[e], sig_t[:, e], a3_t[e][:], MULT)
 
         def partial_of(e, h):
@@ -223,18 +234,17 @@ def tile_moe_bdx_glu_silu_kernel(
         da_coded = {}
 
         def quantize_da(e, h):
-            tag = nsilu_tags[e + 1] if h == 1 and e + 1 < E else f"da_codes{e}{h}"
-            da_codes = keep.tile([P, 2, HALF], U32, name=f"da_codes{e}{h}", tag=tag, align_bytes=64)
-            da_scales = keep.tile([P, 2, HALF], U8, name=f"da_scales{e}{h}", align_bytes=64)
-            for js in (slice(1, 2), slice(0, 1)) if 2 * e + h == HALVES - 1 else (slice(0, 2),):
-                nc.vector.quantize_mx(
-                    out=da_codes[:, js].rearrange("p j n -> p (j n)").bitcast(E4M3X4),
-                    scales=da_scales[:, js].rearrange("p j n -> p (j n)"),
-                    in_=da_of(e, h)[:, js].rearrange("p j n t -> p (j n t)"),
-                )
+            tag = nsilu_tags[e + 1] if h == 1 and e + 1 < E else ""
+            da_codes = held([P, 2, HALF], U32, f"da_codes{e}{h}", tag)
+            da_scales = held([P, 2, HALF], U8, f"da_scales{e}{h}")
+            nc.vector.quantize_mx(
+                out=da_codes[:].rearrange("p j n -> p (j n)").bitcast(E4M3X4),
+                scales=da_scales[:].rearrange("p j n -> p (j n)"),
+                in_=da_of(e, h).rearrange("p j n t -> p (j n t)"),
+            )
             da_coded[2 * e + h] = da_codes, da_scales
 
-        dx_t = [keep.tile([P, S], F32, name=f"dx_t{kt}", tag=f"dy0{kt - 2}" if kt > 2 else f"dx_t{kt}") for kt in range(KT)]
+        dx_t = [held([P, S], F32, f"dx_t{kt}", f"gated{kt}" if kt < NPASS else "") for kt in range(KT)]
 
         def second_product(pool, tag, blocks, halves, copy=nc.scalar.copy):
             acc = pool.tile([P, len(blocks), len(halves), HALF], F32, name=tag)
@@ -256,68 +266,71 @@ def tile_moe_bdx_glu_silu_kernel(
                 by_half = dx_t[kt][:].rearrange("p (h n) -> p h n", n=HALF)
                 copy(out=by_half[:, halves.start : halves.stop : halves.step, :], in_=acc[:, b])
 
-        def combine(pieces):
-            firsts = []
-            for kt, c0, cn in pieces:
-                first = ring3.tile([P, cn], F32, name="first")
-                nc.vector.tensor_copy(first[:], dx_t[kt][:].indirect(pos1_t[:, c0 // 16 : (c0 + cn) // 16]))
-                firsts.append(first)
-            for first, (kt, c0, cn) in zip(firsts, pieces):
-                total = keep.tile([P, cn], F32, name=f"total{kt}_{c0}", tag=f"dy1{kt}" if kt < R - 1 else f"total{kt}_{c0}")
-                nc.vector.tensor_tensor(total[:], dx_t[kt][:].indirect(pos2_t[:, c0 // 16 : (c0 + cn) // 16]), first[:], ADD)
-                nc.sync.dma_start(out=out[kt * P : (kt + 1) * P, c0 : c0 + cn], in_=total[:])
+        def combine(kt, c0, cn, tag=""):
+            first = ring3.tile([P, cn], F32, name="first")
+            nc.scalar.activation(first[:], dx_t[kt][:].indirect(pos1_t[:, c0 // 16 : (c0 + cn) // 16]), ACT.Copy)
+            total = held([P, cn], F32, f"total{kt}_{c0}", tag)
+            nc.vector.tensor_tensor(total[:], dx_t[kt][:].indirect(pos2_t[:, c0 // 16 : (c0 + cn) // 16]), first[:], ADD)
+            nc.sync.dma_start(out=out[kt * P : (kt + 1) * P, c0 : c0 + cn], in_=total[:])
 
-        for t in range(R):
-            for c0, cn in ((0, S),) if t else OPENING:
-                look_up(g_pass0[:, t, c0 : c0 + cn], 0, t, c0, cn)
-        for t in range(R):
-            sigmoid(t)
-        nsilu(0)
-        for c0, cn in CUTS:
-            interleave(0, g_pass0[:, :, c0 : c0 + cn], c0, cn)
-        g_cut = look_up_pass1(*CUTS[0])
-        interleave(1, g_cut[:], *CUTS[0])
-        g_cut = look_up_pass1(*CUTS[1])
-        quantize_g(0, range(0, 1))
-        quantize_g(1, range(0, 1))
-        interleave(1, g_cut[:], *CUTS[1])
-        quantize_g(0, range(1, 2))
-        quantize_g(0, range(2, 4))
-        g_cut = look_up_pass1(*CUTS[2])
-        quantize_g(1, range(1, 2))
-        first_product(0, 0)
-        first_product(0, 1)
-        silu(0)
-        interleave(1, g_cut[:], *CUTS[2])
+        for s in range(NPASS):
+            for t in range(R):
+                for c0, cn in ((0, PAIR),) if s or t else OPENING:
+                    look_up_gated(s, t, c0, cn)
+                look_up_plain(2, s, t)
+                sigmoid(s, t)
+        interleave(0, 0)
+        interleave(0, 1)
+        quantize_g(0, 0)
+        interleave(1, 0)
+        quantize_g(0, 1)
+        interleave(1, 1)
+        quantize_g(1, 0)
+        apply_gate(2, 0)
+        quantize_g(1, 1)
+        apply_gate(2, 1)
+        quantize_g(2, 0)
+        quantize_g(2, 1)
+        prepare(0)
         for e in range(E):
             weigh(e)
             if e + 1 < E:
-                nsilu(e + 1)
-                first_product(e + 1, 0)
-                first_product(e + 1, 1)
-                silu(e + 1)
+                prepare(e + 1)
+            if e == 0:
+                for s in range(NPASS):
+                    for t in range(R):
+                        look_up_plain(3, s, t)
             from_psum(e, 0)
             from_psum(e, 1)
             if e:
                 quantize_da(e - 1, 1)
-            if e == E - 2:
-                for kt in range(EARLY):
+            if e == 2:
+                for kt in range(KT):
                     second_product(psum2, "sum_i", [kt], range(0, 4))
-            if e == E - 1:
-                second_product(psum2, "sum_i", range(EARLY), range(2 * e - 2, 2 * e))
+            if e == 3:
+                for kt in range(0, KT, 2):
+                    second_product(psum4, "turned", [kt, kt + 1], range(4, 6))
             product_da1(e, 0)
-            if e == 0:
-                quantize_g(1, range(2, 4), "a3_t0")
             product_da1(e, 1)
-            quantize_da(e, 0)
+            if e == 1:
+                apply_gate(3, 0, "gate2")
+                quantize_da(e, 0)
+                apply_gate(3, 1)
+                quantize_g(3, 0)
+                quantize_g(3, 1)
+            else:
+                quantize_da(e, 0)
         quantize_da(E - 1, 1)
-        second_product(psum2, "sum_n", range(EARLY), range(HALVES - 2, HALVES - 1))
-        for kt in range(EARLY):
-            second_product(psum4, "turned", [kt], range(HALVES - 1, HALVES), nc.vector.tensor_copy)
-        for pair in range(EARLY, KT, 2):
-            for kt in (pair + 1, pair):
-                second_product(psum4, "turned", [kt], range(1, HALVES, 2))
-                second_product(psum2, "sum_n", [kt], range(0, HALVES, 2))
-        for pair in range(0, KT - 2, 2):
-            combine([(pair, 0, T), (pair + 1, 0, T)])
-        combine([(KT - 2, 0, T), (KT - 1, 0, T - P), (KT - 1, T - P, P)])
+        banks = ((psum2, "sum_n"), (psum2, "sum_n"), (psum2, "sum_i"), (psum2, "sum_i"), (psum4, "turned"), (psum4, "turned"))
+        for kt in range(4):
+            second_product(*banks[kt], [kt], range(6, 8), nc.vector.tensor_copy)
+        combine(0, 0, T // 2, "dy00")
+        combine(0, T // 2, T // 2, "dy01")
+        second_product(*banks[4], [4], range(6, 8))
+        combine(1, 0, T, "dy02")
+        second_product(*banks[5], [5], range(6, 8))
+        combine(2, 0, T, "dy03")
+        combine(3, 0, T, "dy10")
+        combine(4, 0, T, "dy11")
+        combine(5, 0, T - P, "dy12")
+        combine(5, T - P, P, "dy13")

@@ -30,8 +30,9 @@ NPASS = N // (P * R)
 KT = K // P
 RUN = 4
 PAIR = 2 * C
-WIDE = PAIR + 16
-OPENING = ((0, 128), (128, PAIR - 128))
+OWN = PAIR
+WIDE = OWN + 16
+OPENING = ((0, 128), (128, OWN - 128))
 
 
 def tile_moe_bdx_glu_silu_kernel(
@@ -52,8 +53,9 @@ def tile_moe_bdx_glu_silu_kernel(
         pos1_t = keep.tile([P, T // 16], U16, name="pos1_t")
         pos2_t = keep.tile([P, T // 16], U16, name="pos2_t")
         dy = [[held([P, WIDE], F32, f"dy{s}{t}") for t in range(R)] for s in range(NPASS)]
-        gate_pair = held([P, PAIR], F32, "gate_pair")
-        gate_t = {e: held([P, C], F32, f"gate{e}") for e in (2, 3)}
+        gate_pair = held([P, OWN], F32, "gate_pair")
+        lent = {2: (OWN, 3 * C - OWN), 3: (3 * C, C)}
+        gate_t = {e: held([P, lent[e][1]], F32, f"gate{e}") for e in lent}
         a1_t = held([P, R, S], F32, "a1_t")
         a3_t = [held([P, R, C], F32, f"a3_t{e}") for e in range(E)]
         w2_t = held([P, E * NPASS, 2 * H], U8, "w2_t")
@@ -76,9 +78,12 @@ def tile_moe_bdx_glu_silu_kernel(
         def load_gate(queue, dst, c0, cn):
             queue.dma_start(out=dst, in_=gate[0:P, c0 : c0 + cn])
 
-        def load_a1(pair, t):
-            cols = slice(pair * PAIR, (pair + 1) * PAIR)
-            nc.sync.dma_start(out=a1_t[:, t, cols], in_=a1.rearrange("(p t) n -> t p n", t=R)[t][:, cols])
+        def load_a1(queue, t, experts):
+            cols = slice(experts.start * C, experts.stop * C)
+            queue.dma_start(out=a1_t[:, t, cols], in_=a1.rearrange("(p t) n -> t p n", t=R)[t][:, cols])
+
+        a1_pieces = [(0, range(3, 4)), (0, range(2, 3)), (0, range(0, 2))]
+        a1_pieces += [(t, experts) for t in range(1, R) for experts in (range(2, 4), range(0, 2))]
 
         def load_a3(e):
             nc.sync.dma_start(out=a3_t[e][:], in_=a3.rearrange("(p t) n -> p t n", t=R)[:, :, e * C : (e + 1) * C])
@@ -95,20 +100,21 @@ def tile_moe_bdx_glu_silu_kernel(
 
         (c0, cn), (c1, cm) = OPENING
         load_gate(nc.scalar, gate_pair[:, c0 : c0 + cn], c0, cn)
+        load_a1(nc.scalar, *a1_pieces[0])
         load_dy(0, 0)
         nc.sync.dma_start(offs_t[:], offs)
         load_gate(nc.sync, gate_pair[:, c1 : c1 + cm], c1, cm)
         for m in range(NPASS * R):
             if m + 1 < NPASS * R:
                 load_dy(*divmod(m + 1, R))
-            load_a1(*divmod(m, R))
+            load_a1(nc.sync, *a1_pieces[m + 1])
         load_w2(0)
         load_scales(w2s_t, w2_scales)
-        load_gate(nc.sync, gate_t[2][:], 2 * C, C)
+        load_gate(nc.sync, gate_t[2][:], *lent[2])
         load_w2(1)
         load_a3(0)
         load_w2(2)
-        load_gate(nc.sync, gate_t[3][:], 3 * C, C)
+        load_gate(nc.sync, gate_t[3][:], *lent[3])
         load_a3(1)
         load_w2(3)
         load_a3(2)
@@ -125,7 +131,7 @@ def tile_moe_bdx_glu_silu_kernel(
         def rows_by_runs(residue_major):
             return residue_major.rearrange("p t (c i) -> p c t i", i=RUN)
 
-        gated = [held([P, R, PAIR], F32, f"gated{s}") for s in range(NPASS)]
+        gated = [held([P, R, OWN], F32, f"gated{s}") for s in range(NPASS)]
         plain = {}
         g_words = {}
         g_coded = {}
@@ -139,24 +145,28 @@ def tile_moe_bdx_glu_silu_kernel(
             )
 
         def look_up_plain(e, s, t):
+            c0, cn = lent[e]
             if t == 0:
-                plain[e, s] = held([P, R, C], F32, f"plain{e}{s}", f"plain{s}")
-            nc.scalar.activation(plain[e, s][:, t, :], dy[s][t][:].indirect(offs_t[:, e * C // 16 : (e + 1) * C // 16]), ACT.Copy)
+                plain[e, s] = held([P, R, cn], F32, f"plain{e}{s}", f"g_codes1{s}" if e == 3 else "")
+            nc.scalar.activation(plain[e, s][:, t, :], dy[s][t][:].indirect(offs_t[:, c0 // 16 : (c0 + cn) // 16]), ACT.Copy)
+
+        def words_of(e, tag=""):
+            g_words[e] = held([P, NPASS, C, R], BF16, f"g_words{e}", tag)
 
         def interleave(e, s):
-            g_words[e, s] = held([P, C, R], BF16, f"g_words{e}{s}")
-            nc.vector.tensor_copy(by_runs(g_words[e, s][:]), rows_by_runs(gated[s][:, :, e * C : (e + 1) * C]))
+            cn = min(C, OWN - e * C)
+            nc.vector.tensor_copy(by_runs(g_words[e][:, s, :cn]), rows_by_runs(gated[s][:, :, e * C : e * C + cn]))
 
-        def apply_gate(e, s, tag=""):
-            g_words[e, s] = held([P, C, R], BF16, f"g_words{e}{s}", tag)
-            spread = gate_t[e][:].rearrange("p (c i) -> p c i", i=RUN).unsqueeze(2).to_broadcast([P, C // RUN, R, RUN])
-            nc.vector.tensor_tensor(by_runs(g_words[e, s][:]), rows_by_runs(plain[e, s][:]), spread, MULT)
+        def apply_gate(e, s):
+            cn = lent[e][1]
+            spread = gate_t[e][:].rearrange("p (c i) -> p c i", i=RUN).unsqueeze(2).to_broadcast([P, cn // RUN, R, RUN])
+            nc.vector.tensor_tensor(by_runs(g_words[e][:, s, C - cn :]), rows_by_runs(plain[e, s][:]), spread, MULT)
 
         def quantize_g(e, s):
-            codes = held([P, C], U32, f"g_codes{e}{s}")
+            codes = held([P, C], U32, f"g_codes{e}{s}", ("nsilu_odd", "silu_odd")[s] if e == 0 else "")
             scales = held([P, C], U8, f"g_scales{e}{s}")
             nc.vector.quantize_mx(
-                out=codes[:].bitcast(E4M3X4), scales=scales[:], in_=g_words[e, s][:].rearrange("p n t -> p (n t)")
+                out=codes[:].bitcast(E4M3X4), scales=scales[:], in_=g_words[e][:, s].rearrange("p n t -> p (n t)")
             )
             g_coded[e, s] = codes, scales
 
@@ -188,21 +198,23 @@ def tile_moe_bdx_glu_silu_kernel(
         nsilu_tags = ("nsilu_even", "nsilu_odd", "nsilu_even", "a3_t1")
         silu_t = {}
 
-        def sigmoid(pair, t):
-            src = a1_t[:, t, pair * PAIR : (pair + 1) * PAIR].rearrange("p (e n) -> p e n", e=2)
-            nc.scalar.activation(sig_t[:, 2 * pair : 2 * pair + 2, t, :], src, ACT.Sigmoid)
+        def sigmoid(t, experts):
+            src = a1_t[:, t, experts.start * C : experts.stop * C].rearrange("p (e n) -> p e n", n=C)
+            nc.scalar.activation(sig_t[:, experts.start : experts.stop, t, :], src, ACT.Sigmoid)
 
         def nsilu(e):
             nsilu_t[e] = held([P, R, C], F32, f"nsilu_t{e}", nsilu_tags[e])
             nc.scalar.activation(nsilu_t[e][:], a1_t[:, :, e * C : (e + 1) * C], ACT.Silu, scale=-1.0)
 
         def silu(e):
-            silu_t[e] = ring2.tile([P, C, R], F32, name="silu_t")
+            silu_t[e] = held([P, C, R], F32, f"silu_t{e}", ("silu_even", "silu_odd")[e % 2])
             nc.scalar.activation(by_runs(silu_t[e][:]), rows_by_runs(a1_t[:, :, e * C : (e + 1) * C]), ACT.Silu)
 
-        def prepare(e):
+        def factors(e):
             nsilu(e)
             silu(e)
+
+        def first_products(e):
             first_product(e, 0)
             first_product(e, 1)
 
@@ -266,19 +278,34 @@ def tile_moe_bdx_glu_silu_kernel(
                 by_half = dx_t[kt][:].rearrange("p (h n) -> p h n", n=HALF)
                 copy(out=by_half[:, halves.start : halves.stop : halves.step, :], in_=acc[:, b])
 
-        def combine(kt, c0, cn, tag=""):
-            first = ring3.tile([P, cn], F32, name="first")
-            nc.scalar.activation(first[:], dx_t[kt][:].indirect(pos1_t[:, c0 // 16 : (c0 + cn) // 16]), ACT.Copy)
+        def ring_of(turn):
+            return ("sum_i", "sum_n")[turn % 2]
+
+        firsts = {}
+
+        def fetch_first(kt, c0, cn, on_scalar, tag=""):
+            first = held([P, cn], F32, f"first{kt}_{c0}", tag)
+            picked = dx_t[kt][:].indirect(pos1_t[:, c0 // 16 : (c0 + cn) // 16])
+            if on_scalar:
+                nc.scalar.activation(first[:], picked, ACT.Copy)
+            else:
+                nc.vector.tensor_copy(first[:], picked)
+            firsts[kt, c0] = first
+
+        def add_second(kt, c0, cn, tag=""):
             total = held([P, cn], F32, f"total{kt}_{c0}", tag)
-            nc.vector.tensor_tensor(total[:], dx_t[kt][:].indirect(pos2_t[:, c0 // 16 : (c0 + cn) // 16]), first[:], ADD)
+            nc.vector.tensor_tensor(total[:], dx_t[kt][:].indirect(pos2_t[:, c0 // 16 : (c0 + cn) // 16]), firsts[kt, c0][:], ADD)
             nc.sync.dma_start(out=out[kt * P : (kt + 1) * P, c0 : c0 + cn], in_=total[:])
 
+        sigmoid(*a1_pieces[0])
         for s in range(NPASS):
             for t in range(R):
-                for c0, cn in ((0, PAIR),) if s or t else OPENING:
+                for c0, cn in ((0, OWN),) if s or t else OPENING:
                     look_up_gated(s, t, c0, cn)
                 look_up_plain(2, s, t)
-                sigmoid(s, t)
+                sigmoid(*a1_pieces[s * R + t + 1])
+        for e in range(3):
+            words_of(e)
         interleave(0, 0)
         interleave(0, 1)
         quantize_g(0, 0)
@@ -291,29 +318,33 @@ def tile_moe_bdx_glu_silu_kernel(
         apply_gate(2, 1)
         quantize_g(2, 0)
         quantize_g(2, 1)
-        prepare(0)
+        factors(0)
+        first_products(0)
+        factors(1)
+        first_products(1)
+        for s in range(NPASS):
+            for t in range(R):
+                look_up_plain(3, s, t)
         for e in range(E):
             weigh(e)
-            if e + 1 < E:
-                prepare(e + 1)
-            if e == 0:
-                for s in range(NPASS):
-                    for t in range(R):
-                        look_up_plain(3, s, t)
+            if 2 <= e + 1 < E:
+                first_products(e + 1)
+                factors(e + 1)
             from_psum(e, 0)
             from_psum(e, 1)
             if e:
                 quantize_da(e - 1, 1)
             if e == 2:
                 for kt in range(KT):
-                    second_product(psum2, "sum_i", [kt], range(0, 4))
+                    second_product(psum2, ring_of(kt), [kt], range(0, 4))
             if e == 3:
                 for kt in range(0, KT, 2):
-                    second_product(psum4, "turned", [kt, kt + 1], range(4, 6))
+                    second_product(psum2, ring_of(kt // 2), [kt, kt + 1], range(4, 6))
             product_da1(e, 0)
             product_da1(e, 1)
             if e == 1:
-                apply_gate(3, 0, "gate2")
+                words_of(3, "gate2")
+                apply_gate(3, 0)
                 quantize_da(e, 0)
                 apply_gate(3, 1)
                 quantize_g(3, 0)
@@ -321,16 +352,12 @@ def tile_moe_bdx_glu_silu_kernel(
             else:
                 quantize_da(e, 0)
         quantize_da(E - 1, 1)
-        banks = ((psum2, "sum_n"), (psum2, "sum_n"), (psum2, "sum_i"), (psum2, "sum_i"), (psum4, "turned"), (psum4, "turned"))
-        for kt in range(4):
-            second_product(*banks[kt], [kt], range(6, 8), nc.vector.tensor_copy)
-        combine(0, 0, T // 2, "dy00")
-        combine(0, T // 2, T // 2, "dy01")
-        second_product(*banks[4], [4], range(6, 8))
-        combine(1, 0, T, "dy02")
-        second_product(*banks[5], [5], range(6, 8))
-        combine(2, 0, T, "dy03")
-        combine(3, 0, T, "dy10")
-        combine(4, 0, T, "dy11")
-        combine(5, 0, T - P, "dy12")
-        combine(5, T - P, P, "dy13")
+        for kt in range(KT - 1):
+            second_product(psum2, ring_of(kt + 1), [kt], range(6, 8), nc.vector.tensor_copy)
+        spare = ("g_words0", "g_words1", "g_words2", "plain20", "plain21", "a3_t0", "a3_t2")
+        pieces = [(kt, 0, T) for kt in range(KT - 1)] + [(KT - 1, 0, T - P), (KT - 1, T - P, P)]
+        for m, piece in enumerate(pieces):
+            if m == 2:
+                second_product(psum2, ring_of(KT), [KT - 1], range(6, 8))
+            fetch_first(*piece, True, spare[m])
+            add_second(*piece, f"dy{m // R}{m % R}")

@@ -41,7 +41,6 @@ def tile_moe_bdx_glu_silu_kernel(
     nc = tc.nc
     with ExitStack() as ctx:
         keep = ctx.enter_context(tc.tile_pool(name="keep", bufs=1))
-        ring3 = ctx.enter_context(tc.tile_pool(name="ring3", bufs=3))
         ring2 = ctx.enter_context(tc.tile_pool(name="ring2", bufs=2))
         psum2 = ctx.enter_context(tc.psum_pool(name="psum2", bufs=2))
         psum4 = ctx.enter_context(tc.psum_pool(name="psum4", bufs=4))
@@ -150,27 +149,27 @@ def tile_moe_bdx_glu_silu_kernel(
                 plain[e, s] = held([P, R, cn], F32, f"plain{e}{s}", f"g_codes1{s}" if e == 3 else "")
             nc.scalar.activation(plain[e, s][:, t, :], dy[s][t][:].indirect(offs_t[:, c0 // 16 : (c0 + cn) // 16]), ACT.Copy)
 
-        def words_of(e, tag=""):
-            g_words[e] = held([P, NPASS, C, R], BF16, f"g_words{e}", tag)
-
         def interleave(e, s):
-            cn = min(C, OWN - e * C)
-            nc.vector.tensor_copy(by_runs(g_words[e][:, s, :cn]), rows_by_runs(gated[s][:, :, e * C : e * C + cn]))
+            g_words[e, s] = held([P, C, R], BF16, f"g_words{e}{s}")
+            nc.vector.tensor_copy(by_runs(g_words[e, s][:]), rows_by_runs(gated[s][:, :, e * C : (e + 1) * C]))
 
         def apply_gate(e, s):
-            cn = lent[e][1]
-            spread = gate_t[e][:].rearrange("p (c i) -> p c i", i=RUN).unsqueeze(2).to_broadcast([P, cn // RUN, R, RUN])
-            nc.vector.tensor_tensor(by_runs(g_words[e][:, s, C - cn :]), rows_by_runs(plain[e, s][:]), spread, MULT)
+            tag = {(2, 0): "turn_a", (3, 0): "turn_b", (3, 1): "turn_c"}.get((e, s), "")
+            g_words[e, s] = held([P, C, R], BF16, f"g_words{e}{s}", tag)
+            spread = gate_t[e][:].rearrange("p (c i) -> p c i", i=RUN).unsqueeze(2).to_broadcast([P, C // RUN, R, RUN])
+            nc.vector.tensor_tensor(by_runs(g_words[e, s][:]), rows_by_runs(plain[e, s][:]), spread, MULT)
 
         def quantize_g(e, s):
             codes = held([P, C], U32, f"g_codes{e}{s}", ("nsilu_odd", "silu_odd")[s] if e == 0 else "")
             scales = held([P, C], U8, f"g_scales{e}{s}")
             nc.vector.quantize_mx(
-                out=codes[:].bitcast(E4M3X4), scales=scales[:], in_=g_words[e][:, s].rearrange("p n t -> p (n t)")
+                out=codes[:].bitcast(E4M3X4), scales=scales[:], in_=g_words[e, s][:].rearrange("p n t -> p (n t)")
             )
             g_coded[e, s] = codes, scales
 
         dh = {}
+        summed = {}
+        parted_t = {}
 
         def first_product(e, h):
             slots = slice(h * HALF, (h + 1) * HALF)
@@ -186,9 +185,20 @@ def tile_moe_bdx_glu_silu_kernel(
                     start=(s == 0),
                     stop=(s == NPASS - 1),
                 )
+            summed[e, h] = by_slot
+
+        def part(e, h, on_vector=False):
             parted = ring2.tile([P, R, P], F32, name="parted")
-            nc.scalar.activation(parted[:], by_slot[:].rearrange("p (q t) -> p t q", t=R), ACT.Copy, scale=-1.0)
-            turned = psum4.tile([P, R, HALF], F32, name="turned")
+            by_residue = summed[e, h][:].rearrange("p (q t) -> p t q", t=R)
+            if on_vector:
+                nc.vector.tensor_scalar(parted[:], by_residue, -1.0, None, MULT)
+            else:
+                nc.scalar.activation(parted[:], by_residue, ACT.Copy, scale=-1.0)
+            parted_t[e, h] = parted
+
+        def turn(e, h):
+            parted = parted_t[e, h]
+            turned = psum2.tile([P, R, HALF], F32, name="turned")
             for t in range(R):
                 nc.tensor.transpose(turned[:, t, :], parted[:, t, :], ident[:])
             dh[e, h] = turned
@@ -219,67 +229,62 @@ def tile_moe_bdx_glu_silu_kernel(
             first_product(e, 1)
 
         weighed = {}
-        work = {}
+        partial = {}
+        da = {}
 
         def weigh(e):
-            weighed[e] = held([P, R, C], F32, f"weighed{e}", f"gate{2 + e // 2}")[:]
+            weighed[e] = held([P, R, C], F32, f"weighed{e}", ("turn_a", "turn_b", "turn_b", "turn_c")[e])[:]
             nc.gpsimd.tensor_tensor(weighed[e], sig_t[:, e], a3_t[e][:], MULT)
 
-        def partial_of(e, h):
-            return work[e, h][:, : R * HALF].rearrange("p (t n) -> p t n", t=R)
-
-        def da_of(e, h):
-            return work[e, h][:, R * HALF :].bitcast(BF16).rearrange("p (j n t) -> p j n t", j=2, t=R)
-
         def from_psum(e, h):
-            work[e, h] = ring3.tile([P, R * C], F32, name="work", align_bytes=64)
+            partial[e, h] = held([P, R, HALF], F32, f"partial{e}{h}", "turn_c" if (e, h) == (1, 1) else f"partial{h}")
+            if h == 0:
+                da[e, 1] = held([P, C, R], BF16, f"da3_{e}", ("turn_b", "turn_a", "turn_c", "turn_b")[e])
             slots = slice(h * HALF, (h + 1) * HALF)
-            nc.vector.scalar_tensor_tensor(partial_of(e, h), nsilu_t[e][:, :, slots], 1.0, dh[e, h][:], SUB, MULT)
+            nc.vector.scalar_tensor_tensor(partial[e, h][:], nsilu_t[e][:, :, slots], 1.0, dh[e, h][:], SUB, MULT)
             nc.vector.scalar_tensor_tensor(
-                da_of(e, h)[:, 1], silu_t[e][:, slots, :], -1.0, dh[e, h][:].rearrange("p t n -> p n t"), MULT, MULT
+                da[e, 1][:, slots], silu_t[e][:, slots, :], -1.0, dh[e, h][:].rearrange("p t n -> p n t"), MULT, MULT
             )
 
         def product_da1(e, h):
-            factor = weighed[e][:, :, h * HALF : (h + 1) * HALF]
-            nc.vector.tensor_tensor(by_runs(da_of(e, h)[:, 0]), rows_by_runs(partial_of(e, h)), rows_by_runs(factor), MULT)
+            if h == 0:
+                da[e, 0] = held([P, C, R], BF16, f"da1_{e}", "da1")
+            slots = slice(h * HALF, (h + 1) * HALF)
+            nc.vector.tensor_tensor(
+                by_runs(da[e, 0][:, slots]), rows_by_runs(partial[e, h][:]), rows_by_runs(weighed[e][:, :, slots]), MULT
+            )
 
         da_coded = {}
 
-        def quantize_da(e, h):
-            tag = nsilu_tags[e + 1] if h == 1 and e + 1 < E else ""
-            da_codes = held([P, 2, HALF], U32, f"da_codes{e}{h}", tag)
-            da_scales = held([P, 2, HALF], U8, f"da_scales{e}{h}")
+        def quantize_da(e, j):
+            da_codes = held([P, C], U32, f"da_codes{e}{j}")
+            da_scales = held([P, C], U8, f"da_scales{e}{j}")
             nc.vector.quantize_mx(
-                out=da_codes[:].rearrange("p j n -> p (j n)").bitcast(E4M3X4),
-                scales=da_scales[:].rearrange("p j n -> p (j n)"),
-                in_=da_of(e, h).rearrange("p j n t -> p (j n t)"),
+                out=da_codes[:].bitcast(E4M3X4), scales=da_scales[:], in_=da[e, j][:].rearrange("p n t -> p (n t)")
             )
-            da_coded[2 * e + h] = da_codes, da_scales
+            da_coded[e, j] = da_codes, da_scales
 
         dx_t = [held([P, S], F32, f"dx_t{kt}", f"gated{kt}" if kt < NPASS else "") for kt in range(KT)]
 
-        def second_product(pool, tag, blocks, halves, copy=nc.scalar.copy):
-            acc = pool.tile([P, len(blocks), len(halves), HALF], F32, name=tag)
-            for b, kt in enumerate(blocks):
-                for i in reversed(range(len(halves))):
-                    da_codes, da_scales = da_coded[halves[i]]
-                    e = halves[i] // 2
-                    for j in (1, 0):
-                        nc.tensor.matmul_mx(
-                            out=acc[:, b, i, :],
-                            lhsT=w13_t[j][:, e, 2 * P * kt : 2 * P * (kt + 1)].bitcast(E2M1X4),
-                            lhsT_scale=w13s_t[j][:, e, P * kt : P * (kt + 1)],
-                            rhs=da_codes[:, j, :].bitcast(E4M3X4),
-                            rhs_scale=da_scales[:, j, :],
-                            start=(j == 1),
-                            stop=(j == 0),
-                        )
-            for b, kt in enumerate(blocks):
-                by_half = dx_t[kt][:].rearrange("p (h n) -> p h n", n=HALF)
-                copy(out=by_half[:, halves.start : halves.stop : halves.step, :], in_=acc[:, b])
+        def dx_passes(acc, kt, e):
+            for j in (1, 0):
+                da_codes, da_scales = da_coded[e, j]
+                nc.tensor.matmul_mx(
+                    out=acc,
+                    lhsT=w13_t[j][:, e, 2 * P * kt : 2 * P * (kt + 1)].bitcast(E2M1X4),
+                    lhsT_scale=w13s_t[j][:, e, P * kt : P * (kt + 1)],
+                    rhs=da_codes[:].bitcast(E4M3X4),
+                    rhs_scale=da_scales[:],
+                    start=(j == 1),
+                    stop=(j == 0),
+                )
 
-        def ring_of(turn):
-            return ("sum_i", "sum_n")[turn % 2]
+        def second_product(pool, tag, e, blocks, copy):
+            acc = pool.tile([P, len(blocks), C], F32, name=tag)
+            for b, kt in enumerate(blocks):
+                dx_passes(acc[:, b], kt, e)
+            for b, kt in enumerate(blocks):
+                copy(out=dx_t[kt][:, e * C : (e + 1) * C], in_=acc[:, b])
 
         firsts = {}
 
@@ -304,8 +309,6 @@ def tile_moe_bdx_glu_silu_kernel(
                     look_up_gated(s, t, c0, cn)
                 look_up_plain(2, s, t)
                 sigmoid(*a1_pieces[s * R + t + 1])
-        for e in range(3):
-            words_of(e)
         interleave(0, 0)
         interleave(0, 1)
         quantize_g(0, 0)
@@ -318,32 +321,36 @@ def tile_moe_bdx_glu_silu_kernel(
         apply_gate(2, 1)
         quantize_g(2, 0)
         quantize_g(2, 1)
-        factors(0)
+        nsilu(0)
         first_products(0)
-        factors(1)
-        first_products(1)
-        for s in range(NPASS):
-            for t in range(R):
-                look_up_plain(3, s, t)
+        part(0, 0)
+        turn(0, 0)
+        silu(0)
+        part(0, 1)
+        turn(0, 1)
         for e in range(E):
             weigh(e)
-            if 2 <= e + 1 < E:
+            if e + 1 < E:
                 first_products(e + 1)
+                part(e + 1, 0)
                 factors(e + 1)
+            if e == 0:
+                for s in range(NPASS):
+                    for t in range(R):
+                        look_up_plain(3, s, t)
             from_psum(e, 0)
             from_psum(e, 1)
-            if e:
-                quantize_da(e - 1, 1)
-            if e == 2:
-                for kt in range(KT):
-                    second_product(psum2, ring_of(kt), [kt], range(0, 4))
-            if e == 3:
-                for kt in range(0, KT, 2):
-                    second_product(psum2, ring_of(kt // 2), [kt, kt + 1], range(4, 6))
+            if e + 1 < E:
+                turn(e + 1, 0)
+                part(e + 1, 1, True)
+                turn(e + 1, 1)
+            else:
+                for pair in range(0, KT, 2):
+                    second_product(psum4, "sum_i", e - 1, (pair, pair + 1), nc.scalar.copy if pair else nc.vector.tensor_copy)
             product_da1(e, 0)
             product_da1(e, 1)
+            quantize_da(e, 1)
             if e == 1:
-                words_of(3, "gate2")
                 apply_gate(3, 0)
                 quantize_da(e, 0)
                 apply_gate(3, 1)
@@ -351,13 +358,16 @@ def tile_moe_bdx_glu_silu_kernel(
                 quantize_g(3, 1)
             else:
                 quantize_da(e, 0)
-        quantize_da(E - 1, 1)
-        for kt in range(KT - 1):
-            second_product(psum2, ring_of(kt + 1), [kt], range(6, 8), nc.vector.tensor_copy)
-        spare = ("g_words0", "g_words1", "g_words2", "plain20", "plain21", "a3_t0", "a3_t2")
+            if e + 2 < E:
+                for pair in range(0, KT, 2):
+                    second_product(psum4, "sum_i", e, (pair, pair + 1), nc.scalar.copy)
+        late_banks = ((psum2, "sum_n"),) * 2 + ((psum2, "turned"),) * 2 + ((psum4, "sum_i"),) * 2
+        spare = ("g_words00", "g_words01", "g_words10", "plain20", "plain21", "a3_t0", "a3_t2")
         pieces = [(kt, 0, T) for kt in range(KT - 1)] + [(KT - 1, 0, T - P), (KT - 1, T - P, P)]
         for m, piece in enumerate(pieces):
-            if m == 2:
-                second_product(psum2, ring_of(KT), [KT - 1], range(6, 8))
-            fetch_first(*piece, True, spare[m])
+            kt, c0, cn = piece
+            if c0 == 0:
+                second_product(*late_banks[kt], E - 1, (kt,), nc.scalar.copy if kt else nc.vector.tensor_copy)
+            fetch_first(*piece, kt > 0, spare[m])
+        for m, piece in enumerate(pieces):
             add_second(*piece, f"dy{m // R}{m % R}")

@@ -81,8 +81,7 @@ def tile_moe_bdx_glu_silu_kernel(
             cols = slice(experts.start * C, experts.stop * C)
             queue.dma_start(out=a1_t[:, t, cols], in_=a1.rearrange("(p t) n -> t p n", t=R)[t][:, cols])
 
-        a1_pieces = [(0, range(3, 4)), (0, range(2, 3)), (0, range(0, 2))]
-        a1_pieces += [(t, experts) for t in range(1, R) for experts in (range(2, 4), range(0, 2))]
+        a1_pieces = [(0, range(3, 4)), (0, range(0, 3))] + [(t, range(E)) for t in range(1, R)]
 
         def load_a3(e):
             nc.sync.dma_start(out=a3_t[e][:], in_=a3.rearrange("(p t) n -> p t n", t=R)[:, :, e * C : (e + 1) * C])
@@ -103,10 +102,10 @@ def tile_moe_bdx_glu_silu_kernel(
         load_dy(0, 0)
         nc.sync.dma_start(offs_t[:], offs)
         load_gate(nc.sync, gate_pair[:, c1 : c1 + cm], c1, cm)
-        for m in range(NPASS * R):
-            if m + 1 < NPASS * R:
-                load_dy(*divmod(m + 1, R))
-            load_a1(nc.sync, *a1_pieces[m + 1])
+        for m in range(1, NPASS * R):
+            load_dy(*divmod(m, R))
+        for piece in a1_pieces[1:]:
+            load_a1(nc.sync, *piece)
         load_w2(0)
         load_scales(w2s_t, w2_scales)
         load_gate(nc.sync, gate_t[2][:], *lent[2])
@@ -308,7 +307,8 @@ def tile_moe_bdx_glu_silu_kernel(
                 for c0, cn in ((0, OWN),) if s or t else OPENING:
                     look_up_gated(s, t, c0, cn)
                 look_up_plain(2, s, t)
-                sigmoid(*a1_pieces[s * R + t + 1])
+        for piece in a1_pieces[1:]:
+            sigmoid(*piece)
         interleave(0, 0)
         interleave(0, 1)
         quantize_g(0, 0)

@@ -30,8 +30,8 @@ NPASS = N // (P * R)
 KT = K // P
 RUN = 4
 PAIR = 2 * C
-OWN = PAIR
-WIDE = OWN + 16
+OWN = PAIR - 64
+FIRST = 64
 OPENING = ((0, 128), (128, OWN - 128))
 
 
@@ -41,7 +41,6 @@ def tile_moe_bdx_glu_silu_kernel(
     nc = tc.nc
     with ExitStack() as ctx:
         keep = ctx.enter_context(tc.tile_pool(name="keep", bufs=1))
-        ring2 = ctx.enter_context(tc.tile_pool(name="ring2", bufs=2))
         psum2 = ctx.enter_context(tc.psum_pool(name="psum2", bufs=2))
         psum4 = ctx.enter_context(tc.psum_pool(name="psum4", bufs=4))
 
@@ -51,7 +50,7 @@ def tile_moe_bdx_glu_silu_kernel(
         offs_t = keep.tile([P, S // 16], U16, name="offs_t")
         pos1_t = keep.tile([P, T // 16], U16, name="pos1_t")
         pos2_t = keep.tile([P, T // 16], U16, name="pos2_t")
-        dy = [[held([P, WIDE], F32, f"dy{s}{t}") for t in range(R)] for s in range(NPASS)]
+        dy = [[held([P, T], F32, f"dy{s}{t}") for t in range(R)] for s in range(NPASS)]
         gate_pair = held([P, OWN], F32, "gate_pair")
         lent = {2: (OWN, 3 * C - OWN), 3: (3 * C, C)}
         gate_t = {e: held([P, lent[e][1]], F32, f"gate{e}") for e in lent}
@@ -67,21 +66,18 @@ def tile_moe_bdx_glu_silu_kernel(
         nc.gpsimd.memset(w2s_t[:].bitcast(I32), 0)
         nc.gpsimd.memset(w13s_t[0][:].bitcast(I32), 0)
         nc.gpsimd.memset(w13s_t[1][:].bitcast(I32), 0)
-        for window in dy[0] + dy[1]:
-            nc.vector.memset(window[:, T:], 0.0)
 
         def load_dy(s, t):
             rows = dyT[P * R * s : P * R * (s + 1), :].rearrange("(p t) n -> t p n", t=R)
-            nc.sync.dma_start(out=dy[s][t][:, :T], in_=rows[t])
+            nc.sync.dma_start(out=dy[s][t][:], in_=rows[t])
 
         def load_gate(queue, dst, c0, cn):
             queue.dma_start(out=dst, in_=gate[0:P, c0 : c0 + cn])
 
-        def load_a1(queue, t, experts):
-            cols = slice(experts.start * C, experts.stop * C)
-            queue.dma_start(out=a1_t[:, t, cols], in_=a1.rearrange("(p t) n -> t p n", t=R)[t][:, cols])
+        def load_a1(queue, t, c0, cn):
+            queue.dma_start(out=a1_t[:, t, c0 : c0 + cn], in_=a1.rearrange("(p t) n -> t p n", t=R)[t][:, c0 : c0 + cn])
 
-        a1_pieces = [(0, range(3, 4)), (0, range(0, 3))] + [(t, range(E)) for t in range(1, R)]
+        a1_pieces = [(0, S - FIRST, FIRST), (0, S - C, C - FIRST), (0, 0, S - C)] + [(t, 0, S) for t in range(1, R)]
 
         def load_a3(e):
             nc.sync.dma_start(out=a3_t[e][:], in_=a3.rearrange("(p t) n -> p t n", t=R)[:, :, e * C : (e + 1) * C])
@@ -106,9 +102,9 @@ def tile_moe_bdx_glu_silu_kernel(
             load_dy(*divmod(m, R))
         for piece in a1_pieces[1:]:
             load_a1(nc.sync, *piece)
+        load_gate(nc.sync, gate_t[2][:], *lent[2])
         load_w2(0)
         load_scales(w2s_t, w2_scales)
-        load_gate(nc.sync, gate_t[2][:], *lent[2])
         load_w2(1)
         load_a3(0)
         load_w2(2)
@@ -148,18 +144,26 @@ def tile_moe_bdx_glu_silu_kernel(
                 plain[e, s] = held([P, R, cn], F32, f"plain{e}{s}", f"g_codes1{s}" if e == 3 else "")
             nc.scalar.activation(plain[e, s][:, t, :], dy[s][t][:].indirect(offs_t[:, c0 // 16 : (c0 + cn) // 16]), ACT.Copy)
 
+        def words(e, s):
+            if (e, s) not in g_words:
+                tag = {(2, 0): "turn_a", (3, 0): "turn_b", (3, 1): "turn_c"}.get((e, s), "")
+                g_words[e, s] = held([P, C, R], BF16, f"g_words{e}{s}", tag)
+            return g_words[e, s]
+
         def interleave(e, s):
-            g_words[e, s] = held([P, C, R], BF16, f"g_words{e}{s}")
-            nc.vector.tensor_copy(by_runs(g_words[e, s][:]), rows_by_runs(gated[s][:, :, e * C : (e + 1) * C]))
+            cn = min(C, OWN - e * C)
+            nc.vector.tensor_copy(by_runs(words(e, s)[:, :cn]), rows_by_runs(gated[s][:, :, e * C : e * C + cn]))
 
         def apply_gate(e, s):
-            tag = {(2, 0): "turn_a", (3, 0): "turn_b", (3, 1): "turn_c"}.get((e, s), "")
-            g_words[e, s] = held([P, C, R], BF16, f"g_words{e}{s}", tag)
-            spread = gate_t[e][:].rearrange("p (c i) -> p c i", i=RUN).unsqueeze(2).to_broadcast([P, C // RUN, R, RUN])
-            nc.vector.tensor_tensor(by_runs(g_words[e, s][:]), rows_by_runs(plain[e, s][:]), spread, MULT)
+            group = max(e, 2)
+            c0 = max(e * C, OWN)
+            cn = (e + 1) * C - c0
+            cols = slice(c0 - lent[group][0], c0 - lent[group][0] + cn)
+            spread = gate_t[group][:, cols].rearrange("p (c i) -> p c i", i=RUN).unsqueeze(2).to_broadcast([P, cn // RUN, R, RUN])
+            nc.vector.tensor_tensor(by_runs(words(e, s)[:, C - cn :]), rows_by_runs(plain[group, s][:, :, cols]), spread, MULT)
 
         def quantize_g(e, s):
-            codes = held([P, C], U32, f"g_codes{e}{s}", ("nsilu_odd", "silu_odd")[s] if e == 0 else "")
+            codes = held([P, C], U32, f"g_codes{e}{s}", "silu_even" if (e, s) == (0, 1) else "")
             scales = held([P, C], U8, f"g_scales{e}{s}")
             nc.vector.quantize_mx(
                 out=codes[:].bitcast(E4M3X4), scales=scales[:], in_=g_words[e, s][:].rearrange("p n t -> p (n t)")
@@ -187,7 +191,7 @@ def tile_moe_bdx_glu_silu_kernel(
             summed[e, h] = by_slot
 
         def part(e, h, on_vector=False):
-            parted = ring2.tile([P, R, P], F32, name="parted")
+            parted = held([P, R, P], F32, f"parted{e}{h}", ("silu_odd", "nsilu_odd")[h] if e == 0 else f"parted{h}")
             by_residue = summed[e, h][:].rearrange("p (q t) -> p t q", t=R)
             if on_vector:
                 nc.vector.tensor_scalar(parted[:], by_residue, -1.0, None, MULT)
@@ -207,9 +211,11 @@ def tile_moe_bdx_glu_silu_kernel(
         nsilu_tags = ("nsilu_even", "nsilu_odd", "nsilu_even", "a3_t1")
         silu_t = {}
 
-        def sigmoid(t, experts):
-            src = a1_t[:, t, experts.start * C : experts.stop * C].rearrange("p (e n) -> p e n", n=C)
-            nc.scalar.activation(sig_t[:, experts.start : experts.stop, t, :], src, ACT.Sigmoid)
+        def sigmoid(t, c0, cn):
+            width = min(cn, C)
+            src = a1_t[:, t, c0 : c0 + cn].rearrange("p (e n) -> p e n", n=width)
+            dst = sig_t[:, c0 // C : (c0 + cn - 1) // C + 1, t, c0 % C : c0 % C + width]
+            nc.scalar.activation(dst, src, ACT.Sigmoid)
 
         def nsilu(e):
             nsilu_t[e] = held([P, R, C], F32, f"nsilu_t{e}", nsilu_tags[e])
@@ -235,12 +241,15 @@ def tile_moe_bdx_glu_silu_kernel(
             weighed[e] = held([P, R, C], F32, f"weighed{e}", ("turn_a", "turn_b", "turn_b", "turn_c")[e])[:]
             nc.gpsimd.tensor_tensor(weighed[e], sig_t[:, e], a3_t[e][:], MULT)
 
-        def from_psum(e, h):
+        def partial_from_psum(e, h):
             partial[e, h] = held([P, R, HALF], F32, f"partial{e}{h}", "turn_c" if (e, h) == (1, 1) else f"partial{h}")
+            slots = slice(h * HALF, (h + 1) * HALF)
+            nc.vector.scalar_tensor_tensor(partial[e, h][:], nsilu_t[e][:, :, slots], 1.0, dh[e, h][:], SUB, MULT)
+
+        def da3_from_psum(e, h):
             if h == 0:
                 da[e, 1] = held([P, C, R], BF16, f"da3_{e}", ("turn_b", "turn_a", "turn_c", "turn_b")[e])
             slots = slice(h * HALF, (h + 1) * HALF)
-            nc.vector.scalar_tensor_tensor(partial[e, h][:], nsilu_t[e][:, :, slots], 1.0, dh[e, h][:], SUB, MULT)
             nc.vector.scalar_tensor_tensor(
                 da[e, 1][:, slots], silu_t[e][:, slots, :], -1.0, dh[e, h][:].rearrange("p t n -> p n t"), MULT, MULT
             )
@@ -315,6 +324,8 @@ def tile_moe_bdx_glu_silu_kernel(
         interleave(1, 0)
         quantize_g(0, 1)
         interleave(1, 1)
+        apply_gate(1, 0)
+        apply_gate(1, 1)
         quantize_g(1, 0)
         apply_gate(2, 0)
         quantize_g(1, 1)
@@ -325,9 +336,9 @@ def tile_moe_bdx_glu_silu_kernel(
         first_products(0)
         part(0, 0)
         turn(0, 0)
-        silu(0)
         part(0, 1)
         turn(0, 1)
+        silu(0)
         for e in range(E):
             weigh(e)
             if e + 1 < E:
@@ -338,8 +349,9 @@ def tile_moe_bdx_glu_silu_kernel(
                 for s in range(NPASS):
                     for t in range(R):
                         look_up_plain(3, s, t)
-            from_psum(e, 0)
-            from_psum(e, 1)
+            for read in (partial_from_psum, da3_from_psum):
+                read(e, 0)
+                read(e, 1)
             if e + 1 < E:
                 turn(e + 1, 0)
                 part(e + 1, 1, True)

@@ -110,11 +110,11 @@ def tile_moe_bdx_glu_silu_kernel(
         load_w2(2)
         load_gate(nc.sync, gate_t[3][:], *lent[3])
         load_a3(1)
-        load_w2(3)
         load_a3(2)
         for j, (words, scales) in enumerate(((w1_words, w1_scales), (w3_words, w3_scales))):
             nc.sync.dma_start(out=w13_t[j][:].bitcast(I32), in_=words.bitcast(I32).rearrange("e s p n -> p (e s) n"))
             load_scales(w13s_t[j], scales)
+        load_w2(3)
         load_a3(3)
         nc.sync.dma_start(pos1_t[:], pos1)
         nc.sync.dma_start(pos2_t[:], pos2)
@@ -222,7 +222,7 @@ def tile_moe_bdx_glu_silu_kernel(
             nc.scalar.activation(nsilu_t[e][:], a1_t[:, :, e * C : (e + 1) * C], ACT.Silu, scale=-1.0)
 
         def silu(e):
-            silu_t[e] = held([P, C, R], F32, f"silu_t{e}", ("silu_even", "silu_odd")[e % 2])
+            silu_t[e] = held([P, C, R], F32, f"silu_t{e}", ("silu_even", "silu_odd", "silu_even", "g_codes31")[e])
             nc.scalar.activation(by_runs(silu_t[e][:]), rows_by_runs(a1_t[:, :, e * C : (e + 1) * C]), ACT.Silu)
 
         def factors(e):
@@ -238,7 +238,7 @@ def tile_moe_bdx_glu_silu_kernel(
         da = {}
 
         def weigh(e):
-            weighed[e] = held([P, R, C], F32, f"weighed{e}", ("turn_a", "turn_b", "turn_b", "turn_c")[e])[:]
+            weighed[e] = held([P, R, C], F32, f"weighed{e}", ("turn_a", "turn_b", "gate3", "gate3")[e])[:]
             nc.gpsimd.tensor_tensor(weighed[e], sig_t[:, e], a3_t[e][:], MULT)
 
         def partial_from_psum(e, h):
@@ -248,7 +248,7 @@ def tile_moe_bdx_glu_silu_kernel(
 
         def da3_from_psum(e, h):
             if h == 0:
-                da[e, 1] = held([P, C, R], BF16, f"da3_{e}", ("turn_b", "turn_a", "turn_c", "turn_b")[e])
+                da[e, 1] = held([P, C, R], BF16, f"da3_{e}", ("turn_b", "turn_a", "turn_c", "turn_c")[e])
             slots = slice(h * HALF, (h + 1) * HALF)
             nc.vector.scalar_tensor_tensor(
                 da[e, 1][:, slots], silu_t[e][:, slots, :], -1.0, dh[e, h][:].rearrange("p t n -> p n t"), MULT, MULT
@@ -256,7 +256,7 @@ def tile_moe_bdx_glu_silu_kernel(
 
         def product_da1(e, h):
             if h == 0:
-                da[e, 0] = held([P, C, R], BF16, f"da1_{e}", "da1")
+                da[e, 0] = held([P, C, R], BF16, f"da1_{e}", f"da1_{e % 2}")
             slots = slice(h * HALF, (h + 1) * HALF)
             nc.vector.tensor_tensor(
                 by_runs(da[e, 0][:, slots]), rows_by_runs(partial[e, h][:]), rows_by_runs(weighed[e][:, :, slots]), MULT
@@ -265,14 +265,15 @@ def tile_moe_bdx_glu_silu_kernel(
         da_coded = {}
 
         def quantize_da(e, j):
-            da_codes = held([P, C], U32, f"da_codes{e}{j}")
+            da_codes = held([P, C], U32, f"da_codes{e}{j}", "nsilu_even" if (e, j) == (1, 0) else "")
             da_scales = held([P, C], U8, f"da_scales{e}{j}")
             nc.vector.quantize_mx(
                 out=da_codes[:].bitcast(E4M3X4), scales=da_scales[:], in_=da[e, j][:].rearrange("p n t -> p (n t)")
             )
             da_coded[e, j] = da_codes, da_scales
 
-        dx_t = [held([P, S], F32, f"dx_t{kt}", f"gated{kt}" if kt < NPASS else "") for kt in range(KT)]
+        dx_tags = ("gated0", "gated1", "g_codes30", "g_scales30", "g_scales31", "w2s_t")
+        dx_t = {}
 
         def dx_passes(acc, kt, e):
             for j in (1, 0):
@@ -287,12 +288,20 @@ def tile_moe_bdx_glu_silu_kernel(
                     stop=(j == 0),
                 )
 
-        def second_product(pool, tag, e, blocks, copy):
+        def dx_sums(pool, tag, e, blocks):
             acc = pool.tile([P, len(blocks), C], F32, name=tag)
             for b, kt in enumerate(blocks):
                 dx_passes(acc[:, b], kt, e)
+            return acc
+
+        def dx_out(acc, e, blocks, copy):
             for b, kt in enumerate(blocks):
+                if e == 0:
+                    dx_t[kt] = held([P, S], F32, f"dx_t{kt}", dx_tags[kt])
                 copy(out=dx_t[kt][:, e * C : (e + 1) * C], in_=acc[:, b])
+
+        def second_product(pool, tag, e, blocks, copy):
+            dx_out(dx_sums(pool, tag, e, blocks), e, blocks, copy)
 
         firsts = {}
 
@@ -344,36 +353,47 @@ def tile_moe_bdx_glu_silu_kernel(
             if e + 1 < E:
                 first_products(e + 1)
                 part(e + 1, 0)
+                if e == 2:
+                    part(e + 1, 1)
                 factors(e + 1)
             if e == 0:
                 for s in range(NPASS):
                     for t in range(R):
                         look_up_plain(3, s, t)
+            if e == 2:
+                for m, acc in enumerate(early):
+                    dx_out(acc, 0, (2 * m, 2 * m + 1), nc.scalar.copy)
             for read in (partial_from_psum, da3_from_psum):
                 read(e, 0)
                 read(e, 1)
             if e + 1 < E:
                 turn(e + 1, 0)
-                part(e + 1, 1, True)
+                if e < 2:
+                    part(e + 1, 1, True)
                 turn(e + 1, 1)
-            else:
+            if e == 2:
+                quantize_da(1, 0)
                 for pair in range(0, KT, 2):
-                    second_product(psum4, "sum_i", e - 1, (pair, pair + 1), nc.scalar.copy if pair else nc.vector.tensor_copy)
+                    second_product(psum4, "sum_i", 1, (pair, pair + 1), nc.scalar.copy)
+            if e == 3:
+                second_product(psum4, "sum_i", 2, (0,), nc.vector.tensor_copy)
+                second_product(psum4, "sum_i", 2, (1,), nc.scalar.copy)
+                for pair in range(2, KT, 2):
+                    second_product(psum2, "sum_n", 2, (pair, pair + 1), nc.scalar.copy)
             product_da1(e, 0)
             product_da1(e, 1)
-            quantize_da(e, 1)
             if e == 1:
                 apply_gate(3, 0)
-                quantize_da(e, 0)
+                quantize_da(e, 1)
                 apply_gate(3, 1)
                 quantize_g(3, 0)
                 quantize_g(3, 1)
             else:
+                quantize_da(e, 1)
                 quantize_da(e, 0)
-            if e + 2 < E:
-                for pair in range(0, KT, 2):
-                    second_product(psum4, "sum_i", e, (pair, pair + 1), nc.scalar.copy)
-        late_banks = ((psum2, "sum_n"),) * 2 + ((psum2, "turned"),) * 2 + ((psum4, "sum_i"),) * 2
+            if e == 0:
+                early = [dx_sums(psum4, "sum_i", e, (pair, pair + 1)) for pair in range(0, KT, 2)]
+        late_banks = ((psum2, "turned"),) * 2 + ((psum4, "sum_i"),) * 2 + ((psum2, "sum_n"),) * 2
         spare = ("g_words00", "g_words01", "g_words10", "plain20", "plain21", "a3_t0", "a3_t2")
         pieces = [(kt, 0, T) for kt in range(KT - 1)] + [(KT - 1, 0, T - P), (KT - 1, T - P, P)]
         for m, piece in enumerate(pieces):

from contextlib import ExitStack

import concourse.mybir as mybir
from concourse.masks import make_identity

K, T, E, C, H, N = 768, 512, 4, 256, 512, 1024
S = E * C

FLOPS = 2 * S * (N * H + 2 * H * K)
BYTES = 4 * (N * T + 2 * H * S + S + K * T) + E * (N * H // 2 + N * H // 32) + 2 * E * (H * K // 2 + H * K // 32) + 2 * (S + 2 * T) * 8

F32 = mybir.dt.float32
BF16 = mybir.dt.bfloat16
U32 = mybir.dt.uint32
I32 = mybir.dt.int32
U16 = mybir.dt.uint16
U8 = mybir.dt.uint8
E4M3X4 = mybir.dt.float8_e4m3fn_x4
E2M1X4 = mybir.dt.float4_e2m1fn_x4
ACT = mybir.ActivationFunctionType
MULT = mybir.AluOpType.mult
SUB = mybir.AluOpType.subtract
ADD = mybir.AluOpType.add

P = 128
R = 4
HALF = 128
HALVES = S // HALF
NPASS = N // (P * R)
KT = K // P
RUN = 4
PAIR = 2 * C
OWN = PAIR - 64
FIRST = 64
OPENING = ((0, 128), (128, OWN - 128))


def tile_moe_bdx_glu_silu_kernel(
    tc, dyT, a1, a3, w2_words, w2_scales, w1_words, w1_scales, w3_words, w3_scales, gate, offs, pos1, pos2, out
):
    nc = tc.nc
    with ExitStack() as ctx:
        keep = ctx.enter_context(tc.tile_pool(name="keep", bufs=1))
        psum2 = ctx.enter_context(tc.psum_pool(name="psum2", bufs=2))
        psum4 = ctx.enter_context(tc.psum_pool(name="psum4", bufs=4))

        def held(shape, dtype, name, tag=""):
            return keep.tile(shape, dtype, name=name, tag=tag or name, align_bytes=64)

        offs_t = keep.tile([P, S // 16], U16, name="offs_t")
        pos1_t = keep.tile([P, T // 16], U16, name="pos1_t")
        pos2_t = keep.tile([P, T // 16], U16, name="pos2_t")
        dy = [[held([P, T], F32, f"dy{s}{t}") for t in range(R)] for s in range(NPASS)]
        gate_pair = held([P, OWN], F32, "gate_pair")
        lent = {2: (OWN, 3 * C - OWN), 3: (3 * C, C)}
        gate_t = {e: held([P, lent[e][1]], F32, f"gate{e}") for e in lent}
        a1_t = held([P, R, S], F32, "a1_t")
        a3_t = [held([P, R, C], F32, f"a3_t{e}") for e in range(E)]
        w2_t = held([P, E * NPASS, 2 * H], U8, "w2_t")
        w2s_t = held([P, E * NPASS, H], U8, "w2s_t")
        w13_t = [held([P, E, 2 * K], U8, f"w13_t{j}") for j in range(2)]
        w13s_t = [held([P, E, K], U8, f"w13s_t{j}") for j in range(2)]
        ident = held([P, P], F32, "ident")

        make_identity(nc, ident[:])
        nc.gpsimd.memset(w2s_t[:].bitcast(I32), 0)
        nc.gpsimd.memset(w13s_t[0][:].bitcast(I32), 0)
        nc.gpsimd.memset(w13s_t[1][:].bitcast(I32), 0)

        def load_dy(s, t):
            rows = dyT[P * R * s : P * R * (s + 1), :].rearrange("(p t) n -> t p n", t=R)
            nc.sync.dma_start(out=dy[s][t][:], in_=rows[t])

        def load_gate(queue, dst, c0, cn):
            queue.dma_start(out=dst, in_=gate[0:P, c0 : c0 + cn])

        def load_a1(queue, t, c0, cn):
            queue.dma_start(out=a1_t[:, t, c0 : c0 + cn], in_=a1.rearrange("(p t) n -> t p n", t=R)[t][:, c0 : c0 + cn])

        a1_pieces = [(0, S - FIRST, FIRST), (0, S - C, C - FIRST), (0, 0, S - C)] + [(t, 0, S) for t in range(1, R)]

        def load_a3(e):
            nc.sync.dma_start(out=a3_t[e][:], in_=a3.rearrange("(p t) n -> p t n", t=R)[:, :, e * C : (e + 1) * C])

        def load_w2(e):
            src = w2_words.bitcast(I32).rearrange("e s p n -> p (e s) n")
            passes = slice(e * NPASS, (e + 1) * NPASS)
            nc.sync.dma_start(out=w2_t[:, passes, :].bitcast(I32), in_=src[:, passes, :])

        def load_scales(dst, src):
            view = src.bitcast(I32).rearrange("e s (q r) i -> r q (e s) i", r=4)
            for r in range(4):
                nc.sync.dma_start(out=dst[:].bitcast(I32)[r : P : 32, :, :], in_=view[r])

        (c0, cn), (c1, cm) = OPENING
        load_gate(nc.scalar, gate_pair[:, c0 : c0 + cn], c0, cn)
        load_a1(nc.scalar, *a1_pieces[0])
        load_dy(0, 0)
        nc.sync.dma_start(offs_t[:], offs)
        load_gate(nc.sync, gate_pair[:, c1 : c1 + cm], c1, cm)
        for m in range(1, NPASS * R):
            load_dy(*divmod(m, R))
        for piece in a1_pieces[1:]:
            load_a1(nc.sync, *piece)
        load_gate(nc.sync, gate_t[2][:], *lent[2])
        load_w2(0)
        load_scales(w2s_t, w2_scales)
        load_w2(1)
        load_a3(0)
        load_w2(2)
        load_gate(nc.sync, gate_t[3][:], *lent[3])
        load_a3(1)
        load_a3(2)
        for j, (words, scales) in enumerate(((w1_words, w1_scales), (w3_words, w3_scales))):
            nc.sync.dma_start(out=w13_t[j][:].bitcast(I32), in_=words.bitcast(I32).rearrange("e s p n -> p (e s) n"))
            load_scales(w13s_t[j], scales)
        load_w2(3)
        load_a3(3)
        nc.sync.dma_start(pos1_t[:], pos1)
        nc.sync.dma_start(pos2_t[:], pos2)

        def by_runs(slot_major):
            return slot_major.rearrange("p (c i) t -> p c t i", i=RUN)

        def rows_by_runs(residue_major):
            return residue_major.rearrange("p t (c i) -> p c t i", i=RUN)

        gated = [held([P, R, OWN], F32, f"gated{s}") for s in range(NPASS)]
        plain = {}
        g_words = {}
        g_coded = {}

        def look_up_gated(s, t, c0, cn):
            nc.vector.tensor_tensor(
                gated[s][:, t, c0 : c0 + cn],
                dy[s][t][:].indirect(offs_t[:, c0 // 16 : (c0 + cn) // 16]),
                gate_pair[:, c0 : c0 + cn],
                MULT,
            )

        def look_up_plain(e, s, t):
            c0, cn = lent[e]
            if t == 0:
                plain[e, s] = held([P, R, cn], F32, f"plain{e}{s}", f"g_codes1{s}" if e == 3 else "")
            nc.scalar.activation(plain[e, s][:, t, :], dy[s][t][:].indirect(offs_t[:, c0 // 16 : (c0 + cn) // 16]), ACT.Copy)

        def words(e, s):
            if (e, s) not in g_words:
                tag = {(2, 0): "turn_a", (3, 0): "turn_b", (3, 1): "turn_c"}.get((e, s), "")
                g_words[e, s] = held([P, C, R], BF16, f"g_words{e}{s}", tag)
            return g_words[e, s]

        def interleave(e, s):
            cn = min(C, OWN - e * C)
            nc.vector.tensor_copy(by_runs(words(e, s)[:, :cn]), rows_by_runs(gated[s][:, :, e * C : e * C + cn]))

        def apply_gate(e, s):
            group = max(e, 2)
            c0 = max(e * C, OWN)
            cn = (e + 1) * C - c0
            cols = slice(c0 - lent[group][0], c0 - lent[group][0] + cn)
            spread = gate_t[group][:, cols].rearrange("p (c i) -> p c i", i=RUN).unsqueeze(2).to_broadcast([P, cn // RUN, R, RUN])
            nc.vector.tensor_tensor(by_runs(words(e, s)[:, C - cn :]), rows_by_runs(plain[group, s][:, :, cols]), spread, MULT)

        def quantize_g(e, s):
            codes = held([P, C], U32, f"g_codes{e}{s}", "silu_even" if (e, s) == (0, 1) else "")
            scales = held([P, C], U8, f"g_scales{e}{s}")
            nc.vector.quantize_mx(
                out=codes[:].bitcast(E4M3X4), scales=scales[:], in_=g_words[e, s][:].rearrange("p n t -> p (n t)")
            )
            g_coded[e, s] = codes, scales

        dh = {}
        summed = {}
        parted_t = {}

        def first_product(e, h):
            slots = slice(h * HALF, (h + 1) * HALF)
            by_slot = psum2.tile([P, H], F32, name="sum_n")
            for s in range(NPASS):
                codes, scales = g_coded[e, s]
                nc.tensor.matmul_mx(
                    out=by_slot[:],
                    lhsT=codes[:, slots].bitcast(E4M3X4),
                    lhsT_scale=scales[:, slots],
                    rhs=w2_t[:, e * NPASS + s, :].bitcast(E2M1X4),
                    rhs_scale=w2s_t[:, e * NPASS + s, :],
                    start=(s == 0),
                    stop=(s == NPASS - 1),
                )
            summed[e, h] = by_slot

        def part(e, h, on_vector=False):
            parted = held([P, R, P], F32, f"parted{e}{h}", ("silu_odd", "nsilu_odd")[h] if e == 0 else f"parted{h}")
            by_residue = summed[e, h][:].rearrange("p (q t) -> p t q", t=R)
            if on_vector:
                nc.vector.tensor_scalar(parted[:], by_residue, -1.0, None, MULT)
            else:
                nc.scalar.activation(parted[:], by_residue, ACT.Copy, scale=-1.0)
            parted_t[e, h] = parted

        def turn(e, h):
            parted = parted_t[e, h]
            turned = psum2.tile([P, R, HALF], F32, name="turned")
            for t in range(R):
                nc.tensor.transpose(turned[:, t, :], parted[:, t, :], ident[:])
            dh[e, h] = turned

        sig_t = held([P, E, R, C], F32, "sig_t")
        nsilu_t = {}
        nsilu_tags = ("nsilu_even", "nsilu_odd", "nsilu_even", "a3_t1")
        silu_t = {}

        def sigmoid(t, c0, cn):
            width = min(cn, C)
            src = a1_t[:, t, c0 : c0 + cn].rearrange("p (e n) -> p e n", n=width)
            dst = sig_t[:, c0 // C : (c0 + cn - 1) // C + 1, t, c0 % C : c0 % C + width]
            nc.scalar.activation(dst, src, ACT.Sigmoid)

        def nsilu(e):
            nsilu_t[e] = held([P, R, C], F32, f"nsilu_t{e}", nsilu_tags[e])
            nc.scalar.activation(nsilu_t[e][:], a1_t[:, :, e * C : (e + 1) * C], ACT.Silu, scale=-1.0)

        def silu(e):
            silu_t[e] = held([P, C, R], F32, f"silu_t{e}", ("silu_even", "silu_odd", "silu_even", "g_codes31")[e])
            nc.scalar.activation(by_runs(silu_t[e][:]), rows_by_runs(a1_t[:, :, e * C : (e + 1) * C]), ACT.Silu)

        def factors(e):
            nsilu(e)
            silu(e)

        def first_products(e):
            first_product(e, 0)
            first_product(e, 1)

        weighed = {}
        partial = {}
        da = {}

        def weigh(e):
            weighed[e] = held([P, R, C], F32, f"weighed{e}", ("turn_a", "turn_b", "gate3", "gate3")[e])[:]
            nc.gpsimd.tensor_tensor(weighed[e], sig_t[:, e], a3_t[e][:], MULT)

        def partial_from_psum(e, h):
            partial[e, h] = held([P, R, HALF], F32, f"partial{e}{h}", "turn_c" if (e, h) == (1, 1) else f"partial{h}")
            slots = slice(h * HALF, (h + 1) * HALF)
            nc.vector.scalar_tensor_tensor(partial[e, h][:], nsilu_t[e][:, :, slots], 1.0, dh[e, h][:], SUB, MULT)

        def da3_from_psum(e, h):
            if h == 0:
                da[e, 1] = held([P, C, R], BF16, f"da3_{e}", ("turn_b", "turn_a", "turn_c", "turn_c")[e])
            slots = slice(h * HALF, (h + 1) * HALF)
            nc.vector.scalar_tensor_tensor(
                da[e, 1][:, slots], silu_t[e][:, slots, :], -1.0, dh[e, h][:].rearrange("p t n -> p n t"), MULT, MULT
            )

        def product_da1(e, h):
            if h == 0:
                da[e, 0] = held([P, C, R], BF16, f"da1_{e}", f"da1_{e % 2}")
            slots = slice(h * HALF, (h + 1) * HALF)
            nc.vector.tensor_tensor(
                by_runs(da[e, 0][:, slots]), rows_by_runs(partial[e, h][:]), rows_by_runs(weighed[e][:, :, slots]), MULT
            )

        da_coded = {}

        def quantize_da(e, j):
            da_codes = held([P, C], U32, f"da_codes{e}{j}", "nsilu_even" if (e, j) == (1, 0) else "")
            da_scales = held([P, C], U8, f"da_scales{e}{j}")
            nc.vector.quantize_mx(
                out=da_codes[:].bitcast(E4M3X4), scales=da_scales[:], in_=da[e, j][:].rearrange("p n t -> p (n t)")
            )
            da_coded[e, j] = da_codes, da_scales

        dx_tags = ("gated0", "gated1", "g_codes30", "g_scales30", "g_scales31", "w2s_t")
        dx_t = {}

        def dx_passes(acc, kt, e):
            for j in (1, 0):
                da_codes, da_scales = da_coded[e, j]
                nc.tensor.matmul_mx(
                    out=acc,
                    lhsT=w13_t[j][:, e, 2 * P * kt : 2 * P * (kt + 1)].bitcast(E2M1X4),
                    lhsT_scale=w13s_t[j][:, e, P * kt : P * (kt + 1)],
                    rhs=da_codes[:].bitcast(E4M3X4),
                    rhs_scale=da_scales[:],
                    start=(j == 1),
                    stop=(j == 0),
                )

        def dx_sums(pool, tag, e, blocks):
            acc = pool.tile([P, len(blocks), C], F32, name=tag)
            for b, kt in enumerate(blocks):
                dx_passes(acc[:, b], kt, e)
            return acc

        def dx_out(acc, e, blocks, copy):
            for b, kt in enumerate(blocks):
                if e == 0:
                    dx_t[kt] = held([P, S], F32, f"dx_t{kt}", dx_tags[kt])
                copy(out=dx_t[kt][:, e * C : (e + 1) * C], in_=acc[:, b])

        def second_product(pool, tag, e, blocks, copy):
            dx_out(dx_sums(pool, tag, e, blocks), e, blocks, copy)

        firsts = {}

        def fetch_first(kt, c0, cn, on_scalar, tag=""):
            first = held([P, cn], F32, f"first{kt}_{c0}", tag)
            picked = dx_t[kt][:].indirect(pos1_t[:, c0 // 16 : (c0 + cn) // 16])
            if on_scalar:
                nc.scalar.activation(first[:], picked, ACT.Copy)
            else:
                nc.vector.tensor_copy(first[:], picked)
            firsts[kt, c0] = first

        def add_second(kt, c0, cn, tag=""):
            total = held([P, cn], F32, f"total{kt}_{c0}", tag)
            nc.vector.tensor_tensor(total[:], dx_t[kt][:].indirect(pos2_t[:, c0 // 16 : (c0 + cn) // 16]), firsts[kt, c0][:], ADD)
            nc.sync.dma_start(out=out[kt * P : (kt + 1) * P, c0 : c0 + cn], in_=total[:])

        sigmoid(*a1_pieces[0])
        for s in range(NPASS):
            for t in range(R):
                for c0, cn in ((0, OWN),) if s or t else OPENING:
                    look_up_gated(s, t, c0, cn)
                look_up_plain(2, s, t)
        for piece in a1_pieces[1:]:
            sigmoid(*piece)
        interleave(0, 0)
        interleave(0, 1)
        quantize_g(0, 0)
        interleave(1, 0)
        quantize_g(0, 1)
        interleave(1, 1)
        apply_gate(1, 0)
        apply_gate(1, 1)
        quantize_g(1, 0)
        apply_gate(2, 0)
        quantize_g(1, 1)
        apply_gate(2, 1)
        quantize_g(2, 0)
        quantize_g(2, 1)
        nsilu(0)
        first_products(0)
        part(0, 0)
        turn(0, 0)
        part(0, 1)
        turn(0, 1)
        silu(0)
        for e in range(E):
            weigh(e)
            if e + 1 < E:
                first_products(e + 1)
                part(e + 1, 0)
                if e == 2:
                    part(e + 1, 1)
                factors(e + 1)
            if e == 0:
                for s in range(NPASS):
                    for t in range(R):
                        look_up_plain(3, s, t)
            if e == 2:
                for m, acc in enumerate(early):
                    dx_out(acc, 0, (2 * m, 2 * m + 1), nc.scalar.copy)
            for read in (partial_from_psum, da3_from_psum):
                read(e, 0)
                read(e, 1)
            if e + 1 < E:
                turn(e + 1, 0)
                if e < 2:
                    part(e + 1, 1, True)
                turn(e + 1, 1)
            if e == 2:
                quantize_da(1, 0)
                for pair in range(0, KT, 2):
                    second_product(psum4, "sum_i", 1, (pair, pair + 1), nc.scalar.copy)
            if e == 3:
                second_product(psum4, "sum_i", 2, (0,), nc.vector.tensor_copy)
                second_product(psum4, "sum_i", 2, (1,), nc.scalar.copy)
                for pair in range(2, KT, 2):
                    second_product(psum2, "sum_n", 2, (pair, pair + 1), nc.scalar.copy)
            product_da1(e, 0)
            product_da1(e, 1)
            if e == 1:
                apply_gate(3, 0)
                quantize_da(e, 1)
                apply_gate(3, 1)
                quantize_g(3, 0)
                quantize_g(3, 1)
            else:
                quantize_da(e, 1)
                quantize_da(e, 0)
            if e == 0:
                early = [dx_sums(psum4, "sum_i", e, (pair, pair + 1)) for pair in range(0, KT, 2)]
        late_banks = ((psum2, "turned"),) * 2 + ((psum4, "sum_i"),) * 2 + ((psum2, "sum_n"),) * 2
        spare = ("g_words00", "g_words01", "g_words10", "plain20", "plain21", "a3_t0", "a3_t2")
        pieces = [(kt, 0, T) for kt in range(KT - 1)] + [(KT - 1, 0, T - P), (KT - 1, T - P, P)]
        for m, piece in enumerate(pieces):
            kt, c0, cn = piece
            if c0 == 0:
                second_product(*late_banks[kt], E - 1, (kt,), nc.scalar.copy if kt else nc.vector.tensor_copy)
            fetch_first(*piece, kt > 0, spare[m])
        for m, piece in enumerate(pieces):
            add_second(*piece, f"dy{m // R}{m % R}")
